import numpy as np, ml_dtypes
CORES = [6,15,38,47]
N = 4
BF = ml_dtypes.bfloat16
def gentries(a):
    return np.ascontiguousarray(a.reshape(8, 16, -1).transpose(0, 2, 1)).reshape(8, -1)
def gtable(e):
    e = np.asarray(e); return np.ascontiguousarray(e.reshape(8, -1, 16).transpose(0, 2, 1)).reshape(128, -1).astype(np.int32)
W, LW, C, B, KEYS, Q, RO = 4096, 12, 256, 16, 16, 9, 3
def pick(T, c):
    L = np.ascontiguousarray(c.transpose(0, 1, 3, 2)).reshape(N * 8, 16 * C)
    return np.stack([np.take(a, l, axis=1) for a, l in zip(T.reshape(N * 8, 16, W), L)]).reshape(N, 8, 16, C, 16)
def ask(D, X, c, y, w):
    d = pick(D, c); same = (d & (KEYS - 1)) == (c & (KEYS - 1))[..., None]
    cp = np.maximum(c, np.max(np.where(same, d, 0), axis=4))
    x = pick(X, cp); z = (np.max(x, axis=4) + np.min(x, axis=4)) >> 1
    u = np.add.reduce(w * z, axis=2, keepdims=True) & 4095
    return cp, z, u, B * np.arange(C) + (u & (B - 1)), np.abs(z - y)
def put(T, pl, val):
    np.put_along_axis(T, pl, val, axis=3)
def far(X, cp, v):
    return np.add.reduce(np.abs(pick(X, cp) - v[..., None]), axis=2)
def eve(D, X, c, y, w):
    cp, z, u, pl, v = ask(D, X, c, y, w); X = X.copy(); put(X, pl, v)
    return np.sort(far(X, np.roll(cp, 1, axis=0), np.roll(v, 1, axis=0)), axis=-1)[..., Q - 1]
def level(rng, q):
    return np.take_along_axis(np.sort(q, axis=-1), rng.integers(C // 4, 3 * C // 4, (N, 8, 1)), 2)[..., 0]
def sums(rng, tot):
    a = (tot[:, None, :] + np.arange(16).reshape(16, 1)) >> 4; hi, lo = a[:, :8], a[:, 8:]
    e = np.floor(rng.random((N, 8, C)) * (np.minimum(255 - hi, lo) + 1)).astype(np.int64)
    return rng.permuted(np.concatenate([hi + e, lo - e], axis=1), axis=1)
def parts(rng):
    D = rng.integers(0, W, (N, 8, 16, W)); X = (rng.random((N, 8, 16, W)) * rng.integers(64, 257, (N, 8, 1, W))).astype(np.int64)
    c = rng.integers(0, W, (N, 8, 16, C)); y = rng.integers(0, 256, (N, 8, 16, C)); w = rng.integers(0, 16, (N, 8, 16, C)); m = rng.integers(0, 2048, (N, 8, 16, 1))
    return D, X, c, y, w, m
def pack(D, X, c, y, w, m, th):
    return {"rec": (W * X + D).reshape(N, 128, W).astype(np.int32), "req": np.stack([gtable(a.transpose(0, 2, 1).reshape(8, 16 * C)) for a in c]),
            "aim": y.reshape(N, 128, C).astype(np.float32).astype(BF), "wt": w.reshape(N, 128, C).astype(np.float32).astype(BF),
            "mul": m.reshape(N, 128, 1).astype(np.int32), "th": np.repeat(th, 16, axis=1).reshape(N, 128, 1).astype(np.int32)}
def setup_inputs(rng):
    D, X, c, y, w, m = parts(rng)
    return pack(D, X, c, y, w, m, level(rng, eve(D, X, c, y, w)))
def setup_inputs_ties(rng):
    D, X, c, y, w, m = parts(rng); h = C // 2
    put(D, c[..., h:], (c[..., h:] + KEYS) & (W - 1)); put(D, c[..., :h], c[..., :h])
    z = ask(D, X, c, y, w)[1]
    y = np.where(rng.random((N, 8, 1, C)) < 0.3, np.minimum(np.maximum(z + rng.integers(-1, 2, z.shape), 0), 255), y)
    th = level(rng, eve(D, X, c, y, w)) + ((np.arange(8) + np.arange(N)[:, None]) & 1)
    return pack(D, X, c, y, w, m, th)
def setup_inputs_alike(rng):
    D, X, c, y, w, m = parts(rng)
    D[:, 1::2] += KEYS // 2 - (D[:, 1::2] & (KEYS - 1)); c[:, 1::2] += KEYS // 2 - (c[:, 1::2] & (KEYS - 1))
    c[:, 0] = rng.choice(np.array([0, W - 1, W // 2, 5]), (N, 16, C)); c[:, 4] = rng.choice(np.array([0, W - 1, W - 2, KEYS - 1, 7 * KEYS - 1]), (N, 16, C)); c[:, 6] = c[:, 6, :1]
    D[:, 2] = np.arange(W); D[:, 4] = W - 1; D[:, 6] = 0
    X[:, 4] = 255 * rng.integers(0, 2, (N, 1, W))
    return pack(D, X, c, y, w, m, level(rng, eve(D, X, c, y, w)))
def setup_inputs_ends(rng):
    D, X, c, y, w, m = parts(rng)
    th = rng.choice(np.array([0, 1, 4080, 4081]), (N, 8)); q = rng.permutation(N); th[q[0]] = 4081; th[q[1]] = 0
    w[:, 1] = 0
    X[:, 3, :2] = 255; X[:, 3, 2] = 15; w[:, 3] = 0; w[:, 3, 0] = 15; w[:, 3, 1:3] = 1; m[:, 3] = 2047
    y[:, 5] = 255 * rng.integers(0, 2, (N, 16, C)); w[:, 5] = 15; m[:, 5] = 0
    X[:, 7] = 255; y[:, 7] = 255; th[:, 7] = 4080 + (np.arange(N) & 1)
    return pack(D, X, c, y, w, m, th)
def setup_inputs_own(rng):
    D, X, c, y, w, m = parts(rng); lim = 4 * int(rng.integers(513, 1000)) + int(rng.integers(0, 2))
    X[:, :2, :, 1::2] = 255; c[:, :2] |= 1; w[:, :2] = w[:, :2, :1]
    y[:, 0] = sums(rng, rng.choice(np.array([0, 0, 1, 16]), (N, C))); y[:, 1] = sums(rng, lim + rng.integers(-2, 2, (N, C)))
    X[:, 2] = 255 - rng.integers(0, 17, (N, 16, W)); w[:, 2] = 14 + rng.integers(0, 2, (N, 16, C)); y[:, 2] = y[:, 2] * rng.integers(0, 2, (N, 1, C))
    for g, h in ((3, 127), (4, C - 1), (5, int(rng.choice(np.array([32, 63, 64, C // 2, C - 2]))))):
        D[:, g] = B * h; w[:, g] = 0; c[:, g] = KEYS * rng.integers(0, B * h // KEYS + 1, (N, 16, C))
        b = np.tile(rng.integers(0, 2, (1, 16)), (N, 1)); b[np.arange(N), rng.permutation(16)[:N]] ^= 1
        X[:, g, :, B * h] = KEYS * b; y[:, g] = KEYS * rng.integers(0, 2, (N, 16, C)); y[:, g, :, h] = KEYS
    c[:, 6, :, ::2] = 0; D[:, 6, :, 0] = 0; X[:, 6, :, 0] = 0; y[:, 6, :, 0] = 0
    D[:, 7] = np.arange(W); c[:, 7] = (B * (np.arange(C) + rng.integers(-1, 2, (N, 16, C))) + rng.integers(0, B, (N, 16, C))) & (W - 1)
    th = level(rng, eve(D, X, c, y, w))
    th[:, 0] = (np.arange(N) + int(rng.integers(0, 2))) & 1; th[:, 1] = lim; th[:, 3:6] = 8 * KEYS; th[:, 6] = rng.integers(1900, 2200, N)
    return pack(D, X, c, y, w, m, th)
def setup_inputs_spread(rng):
    D, X, c, y, w, m = parts(rng)
    def uneven(*shape):
        a = np.exp2(LW * rng.random(shape)).astype(np.int64) - 1
        return np.where(rng.random(shape[:-2] + (1, shape[-1])) < 0.5, a, W - 1 - a)
    D = np.where(rng.random((N, 8, 1, W)) < 0.5, uneven(N, 8, 16, W), D); c = np.where(rng.random((N, 8, 1, C)) < 0.5, uneven(N, 8, 16, C), c)
    X = (np.exp2(8 * rng.random((N, 8, 1, W))) * rng.random((N, 8, 16, W))).astype(np.int64)
    y = (np.exp2(8 * rng.random((N, 8, 1, C))) * rng.random((N, 8, 16, C))).astype(np.int64); w = w * (rng.random(w.shape) < rng.random((N, 8, 1, C)))
    m = (np.exp2(11 * rng.random(m.shape))).astype(np.int64)
    return pack(D, X, c, y, w, np.minimum(m, 2047), level(rng, eve(D, X, c, y, w)))
def check_inputs(d):
    bad = []
    for k, lo, hi in (("rec", 0, 256 * W - 1), ("req", 0, W - 1), ("aim", 0, 255), ("wt", 0, 15), ("mul", 0, 2047), ("th", 0, 4081)):
        a = np.asarray(d[k]).astype(np.float64)
        if not (np.min(a) >= lo and np.max(a) <= hi): bad.append("range of " + k)
        if not np.all(a == np.floor(a)): bad.append("whole numbers in " + k)
    a = np.asarray(d["th"]).reshape(N, 8, 16)
    if np.any(a != a[:, :, :1]): bad.append("th alike in the rows of a group")
    return bad
def reference(rec, req, aim, wt, mul, th):
    R = rec.astype(np.int64).reshape(N, 8, 16, W); D = R & (W - 1); X = R >> LW
    c = req.astype(np.int64).reshape(N, 8, 16, C)
    y = aim.astype(np.int64).reshape(N, 8, 16, C); w = wt.astype(np.int64).reshape(N, 8, 16, C)
    m = mul.astype(np.int64).reshape(N, 8, 16, 1); lim = th.astype(np.int64).reshape(N, 8, 16)[:, :, 0]
    odd = 2 * np.arange(16).reshape(16, 1) + 1
    for t in range(RO):
        cp, z, u, pl, v = ask(D, X, c, y, w)
        put(D, pl, cp); put(X, pl, v)
        sh = 1 + t % (N - 1)
        ca = np.roll(cp, sh, axis=0); va = np.roll(v, sh, axis=0); pa = np.roll(pl, sh, axis=0)
        near = np.add.reduce((far(X, ca, va) < lim[:, :, None, None]).astype(np.int64), axis=3)
        ok = (near >= Q)[:, :, None, :]
        put(D, pa, np.where(ok, ca, np.take_along_axis(D, pa, 3))); put(X, pa, np.where(ok, va, np.take_along_axis(X, pa, 3)))
        c = (((u * u) >> 5) + m * u + odd * z) & (W - 1)
    return {"yc": c.reshape(N, 128, C).astype(np.float32), "yz": z.reshape(N, 128, C).astype(np.float32).astype(BF), "yx": X.reshape(N, 128, W).astype(np.float32).astype(BF)}

@@ -1,0 +1,477 @@
+from concourse.mybir import dt, AluOpType, AxisListType, ActivationFunctionType
+
+A = AluOpType
+F = ActivationFunctionType
+STEPS = 3
+W = 4096
+WP = W + 256
+C1 = [(0, 64), (64, 128), (128, 192), (192, 256)]
+C3 = [(0, 64), (64, 128), (128, 192), (192, 256)]
+SC = {128: 0, 256: 128}
+SV = {128: 0, 256: 128}
+AC = (2,)
+KG = {2: 0, 3: 3}
+BC0 = [(0, 128, "v"), (128, 256, "g")]
+BCN = [(0, 128, "v"), (128, 256, "g")]
+UNP = [512, 512, 1024, 1024, 1024]
+GAM, SCT, CYC, PEC, LAT, WIN = 1.5, 3.5, 0.000833, 0.00042, 0.08, 0.2
+SND, ARR = 1.2, 3.5
+PRI = {"vMXA.12": -1, "vMN.12": -3, "vU1.12": -5, "vWZ.0": -5, "sHB.512": 5, "sHB.3072": 6, "gCKB.8": -11, "sHB.2048": 6,
+       "sA1.3584": 8, "sHB.2560": -1, "vMX.12": -4, "vMI.12": -5, "vTT.4": -6, "tps3.6": 5, "sXX.3": 12, "tps3.14": -7,
+       "sXG.12": -12, "vZ.8": -9, "vZ.4": 4, "vZ.12": -15, "vCP.12": -6, "sVN.0": -10, "tps4.24": 5}
+ORDER = {}
+
+SCRATCH = {"b%d" % _b: ("psum", [128, 512], "float32") for _b in range(8)}
+
+
+def _sb(cols, dtype, names):
+    for n in names.split():
+        SCRATCH[n] = ("sbuf", [128, cols], dtype)
+
+
+_sb(W, "int32", "REC")
+_sb(W, "float32", "A2 D7 A1")
+_sb(W, "bfloat16", "HB CKB U1 AB MN XG MX MI XA MXA")
+_sb(WP, "float32", "TT")
+_sb(WP, "bfloat16", "XX")
+_sb(256, "int32", "REQ RP CC KK A32 UI UU SQ FF")
+_sb(256, "bfloat16", "AIM WT KM M2 Z H16 HZ FL")
+_sb(256, "float16", "WZ UM C2K")
+_sb(256, "float32", "YC")
+_sb(256, "uint16", "C16")
+_sb(1, "int32", "MUL TH")
+_sb(1, "float32", "THH KF ODC")
+_sb(2048, "bfloat16", "ONES SELA SELC SELB SELM")
+_sb(2048, "float16", "SELH")
+_sb(128, "bfloat16", "BM0 BM BMH IDP IDN IDK IDM IDH IDQ ID4 ID7 OD")
+_sb(128, "float16", "KD BH")
+_sb(1024, "bfloat16", "MSN MSX")
+_sb(16, "int32", "PRI PR I256 I16 R16 N32 N15")
+_sb(16, "float32", "BASE DUM DMC PDC PI PD OF OG")
+_sb(16, "uint16", "P16 O16")
+for _t in range(STEPS):
+    _sb(256, "uint16", "CP%d CA%d" % (_t, _t))
+    _sb(256, "float32", "TV%d TA%d" % (_t, _t))
+    _sb(272, "bfloat16", "VN%d VA%d" % (_t, _t))
+SEMAPHORES = ["sv", "ss", "st", "sg"] + ["d%d" % k for k in range(16)] + \
+    ["%s%d%s" % (m, t, x) for m in ("c", "e", "t", "v", "w") for t in range(STEPS) for x in ("l", "r")]
+
+
+def tk(name, lo, hi):
+    return [(name, u) for u in range(lo // 16, (hi + 15) // 16)]
+
+
+def plan(ops):
+    lw, rd, bk = {}, {}, {}
+    preds = []
+    for i in range(len(ops)):
+        o = ops[i]
+        d = {}
+
+        def need(j, sync):
+            if j != i:
+                d[j] = d.get(j, False) or sync
+        for j in o["after"]:
+            need(j, False)
+        for r in o["R"]:
+            if r in lw:
+                need(lw[r], True)
+        for w in o["W"]:
+            if w in lw:
+                need(lw[w], True)
+            for j in rd.get(w, ()):
+                need(j, ops[j]["e"] != o["e"] or ops[j]["k"] != "c")
+        for b in o["B"]:
+            for e, j in bk.get(b, {}).items():
+                need(j, e != o["e"])
+        for r in o["R"]:
+            rd.setdefault(r, []).append(i)
+        for w in o["W"]:
+            lw[w] = i
+            rd[w] = []
+        for b in o["B"]:
+            bk.setdefault(b, {})[o["e"]] = i
+        preds.append(d)
+    return preds
+
+
+def schedule(ops, preds):
+    n = len(ops)
+    succ = [[] for _ in range(n)]
+    for i in range(n):
+        for j in preds[i]:
+            succ[j].append(i)
+    bl = [0.0] * n
+    for i in range(n - 1, -1, -1):
+        bl[i] = ops[i]["dur"] + max([bl[j] + LAT for j in succ[i]] + [0.0])
+    bl = [bl[i] + PRI.get(ops[i]["tag"], 0.0) for i in range(n)]
+    cnt = [len(preds[i]) for i in range(n)]
+    rdy = [0.0] * n
+    free = {}
+    avail = [i for i in range(n) if cnt[i] == 0]
+    order, start = [], [0.0] * n
+    end = 0.0
+    while avail:
+        best = None
+        for i in avail:
+            s = max(rdy[i], free.get(ops[i]["e"], 0.0))
+            if best is None or s < best:
+                best, e = s, ops[i]["e"]
+        c = [i for i in avail if ops[i]["e"] == e and max(rdy[i], free.get(e, 0.0)) <= best + WIN]
+        i = max(c, key=lambda x: (bl[x], -x))
+        avail.remove(i)
+        s = max(rdy[i], free.get(e, 0.0))
+        start[i] = s
+        if e != "n":
+            free[e] = s + ops[i]["occ"]
+        f = s + ops[i]["dur"]
+        end = max(end, f)
+        order.append(i)
+        for j in succ[i]:
+            cnt[j] -= 1
+            rdy[j] = max(rdy[j], f + LAT if preds[j][i] else s)
+            if cnt[j] == 0:
+                avail.append(j)
+    return order, start, end
+
+
+def build(g, T, core, topo):
+    ops = []
+    q = {"v": g.vector, "s": g.scalar, "t": g.tensor, "g": g, "y": g.sync}
+    t_ = T
+
+    def add(e, calls, cost, R, W_, B=(), k="c", occ=None, sem=None, val=0, after=()):
+        R, W_ = list(R), list(W_)
+        w0 = W_[0]
+        if isinstance(w0, tuple):
+            u = w0[1]
+            nm = w0[0] if isinstance(w0[0], str) else w0[0][0]
+            if nm == "ps":
+                nm = "ps%d" % u
+                u = len(calls) + (sorted(x[1] for x in R if x[0] in ("M2", "MX", "Z", "WZ", "XA", "MXA", "FL")) + [0])[0]
+            w0 = "%s.%s" % (nm, u)
+        ops.append({"tag": e + w0, "e": e, "f": calls, "dur": cost, "occ": cost if occ is None else occ, "R": R, "W": W_,
+                    "B": list(B), "k": k, "sem": sem, "val": val, "after": list(after)})
+
+    def vts(out, i, s1, s2, op0, op1, n, R, W_, B=(), rate=1.0):
+        if op1 is None:
+            f = lambda: g.vector.tensor_scalar(out, i, s1, None, op0)
+        else:
+            f = lambda: g.vector.tensor_scalar(out, i, s1, s2, op0, op1)
+        add("v", [f], max(64, n * rate) * CYC, R, W_, B)
+
+    def vtt(out, a, b, op, n, R, W_, B=(), rate=2.0):
+        add("v", [lambda: g.vector.tensor_tensor(out, a, b, op)], max(64, n * rate) * CYC, R, W_, B)
+
+    def vcp(out, i, n, R, W_, B=(), rate=1.0):
+        add("v", [lambda: g.vector.tensor_copy(out, i)], max(64, n * rate) * CYC, R, W_, B)
+
+    def vset(ap, c, n, W_):
+        add("v", [lambda: g.vector.memset(ap, c)], max(64, n) * CYC, (), W_)
+
+    def vscan(out, m, i, op0, op1, n, R, W_):
+        add("v", [lambda: g.vector.tensor_tensor_scan(out, m, i, 0.0, op0, op1)], n * 0.5 * CYC, R, W_)
+
+    def act(out, i, fn, n, R, W_, B=(), bias=0.0, scale=1.0):
+        add("s", [lambda: g.scalar.activation(out, i, fn, bias=bias, scale=scale)], max(64, n) * CYC + 0.02, R, W_, B)
+
+    def sgat(out, i, n, R, W_):
+        add("s", [lambda: g.scalar.activation(out, i, F.Copy)], n * GAM * CYC + 0.065, R, W_)
+
+    def vscat(out, i, n, R, W_):
+        add("v", [lambda: g.vector.tensor_copy(out, i)], n * SCT * CYC + 0.05, R, W_)
+
+    def mm(lst, R, b):
+        fs = [(lambda o=o, l=l, r=r, s=s, p=p: g.tensor.matmul(o, l, r, s, p)) for (o, l, r, n, s, p) in lst]
+        add("t", fs, sum(max(64, x[3]) for x in lst) * PEC + 0.03, R, [("ps", b)], [b])
+
+    nd = [0]
+
+    def dma(e, out, i, cost, R, W_):
+        s = "d%d" % nd[0]
+        nd[0] += 1
+        add(e, [lambda: q[e].dma_start(out, i)], cost, R, W_, (), "d", 0.1, s, 16)
+
+    def spread(lo, hi, e):
+        n = hi - lo
+        fs = []
+        for j in range(16):
+            o, i = t_.CKB[:, 16 * lo + j:16 * hi:16], t_.KM[:, lo:hi]
+            if e == "v":
+                fs.append(lambda o=o, i=i: g.vector.tensor_copy(o, i))
+            else:
+                fs.append(lambda o=o, i=i: g.affine_select(o, i, [[0, n]], A.is_equal, 0.0, 0, 0))
+        c = {"v": max(64, n * 0.5) * CYC, "g": 0.17 + 2 * n * CYC}[e]
+        add(e, fs, 16 * c, tk("KM", lo, hi), tk("CKB", lo, hi))
+
+    UB = [sum(UNP[:k]) for k in range(len(UNP) + 1)]
+    dma("y", t_.REQ[:], t_.req[:], 2.2, (), ["REQ"])
+    for k in range(len(UNP)):
+        sl = slice(UB[k], UB[k + 1])
+        dma("s" if k % 2 == 0 else "y", t_.REC[:, sl], t_.rec[:, sl], 2.0 + UB[k + 1] * 0.0016, (), [("REC", k)])
+    dma("y", t_.MUL[:], t_.mul[:], 9.0, (), ["MUL"])
+    dma("y", t_.TH[:], t_.th[:], 9.0, (), ["TH"])
+    dma("s", t_.WT[:], t_.wt[:], 9.0, (), ["WT"])
+    dma("s", t_.AIM[:], t_.aim[:], 9.0, (), ["AIM"])
+
+    vset(t_.ONES[:], 1.0, 1024, ["ONES"])
+    vset(t_.MSN[:], 0.0, 512, ["MSN"])
+    vset(t_.MSX[:], 1.0, 512, ["MSX"])
+    vset(t_.MSN[:, 0:1024:16], 65536.0, 64, ["MSN"])
+    vset(t_.MSX[:, 0:1024:16], 0.0, 64, ["MSX"])
+    vset(t_.C2K[:], 2048.0, 256, ["C2K"])
+
+    def gsel(out, i, pat, op, base, cm, n, R, W_):
+        add("g", [lambda: g.affine_select(out, i, pat, op, 0.0, base, cm)], 0.17 + 2 * n * CYC, R, W_)
+
+    def gio(out, pat, base, cm, W_):
+        add("g", [lambda: g.iota(out, pat, base, cm)], 0.16, (), W_)
+    gsel(t_.IDP[:], t_.ONES[:, 0:128], [[-1, 128]], A.is_equal, 0, 1, 128, ["ONES"], ["IDP"])
+    gsel(t_.BM0[:], t_.ONES[:, 0:128], [[-16, 8], [0, 16]], A.is_ge, 0, 1, 128, ["ONES"], ["BM0"])
+    gsel(t_.BM[:], t_.BM0[:], [[16, 8], [0, 16]], A.is_ge, 15, -1, 128, ["BM0"], ["BM"])
+    gio(t_.PRI[:], [[0, 16]], 0, 1, ["PRI"])
+    gio(t_.I256[:], [[256, 16]], 0, 0, ["I256"])
+    gio(t_.I16[:], [[16, 16]], W, 0, ["I16"])
+    gsel(t_.SELA[:], t_.ONES[:], [[1, 16], [0, 8], [-1, 16]], A.is_equal, 0, 0, 2048, ["ONES"], ["SELA"])
+    gsel(t_.SELC[:], t_.SELA[:], [[0, 16], [-16, 8], [0, 16]], A.is_ge, 0, 1, 2048, ["SELA"], ["SELC"])
+    gsel(t_.SELB[:], t_.SELC[:], [[0, 16], [16, 8], [0, 16]], A.is_ge, 15, -1, 2048, ["SELC"], ["SELB"])
+    for nm, c in (("ID4", 4096.0), ("ID7", 7.5), ("IDN", -1.0), ("IDK", 2.0 ** -13), ("IDM", -(2.0 ** -13)), ("IDH", 0.5),
+                  ("IDQ", -0.25)):
+        act(t_[nm][:], t_.IDP[:], F.Copy, 128, ["IDP"], [nm], scale=c)
+    act(t_.BMH[:], t_.BM[:], F.Copy, 128, ["BM"], ["BMH"], scale=-0.5)
+
+    def forms():
+        vts(t_.CC[:], t_.RP[:], 4095, None, A.bitwise_and, None, 256, ["RP"], ["CC"])
+        vts(t_.C16[:], t_.CC[:], -1.0, 4095.0, A.mult, A.add, 256, ["CC"], ["C16"])
+        vts(t_.KK[:], t_.RP[:], 15, None, A.bitwise_and, None, 256, ["RP"], ["KK"])
+        vts(t_.KM[:], t_.KK[:], -1.0, 15.0, A.mult, A.add, 256, ["KK"], tk("KM", 0, 256))
+        vts(t_.A32[:], t_.RP[:], 4080, None, A.bitwise_and, None, 256, ["RP"], ["A32"])
+
+    vts(t_.RP[:], t_.REQ[:], -1.0, -1.0, A.mult, A.add, 256, ["REQ"], ["RP"])
+    forms()
+    for lo, hi, e in BC0:
+        spread(lo, hi, e)
+
+    nb = [0]
+    for k in range(len(UNP)):
+        sl, n = slice(UB[k], UB[k + 1]), UNP[k]
+        vts(t_.A2[:, sl], t_.REC[:, sl], -2047.5, 1.5 * 2.0 ** 35, A.add, A.add, n, [("REC", k)], [("A2", k)])
+        act(t_.XX[:, sl], t_.A2[:, sl], F.Identity, n, [("A2", k)], [("XX", k)], bias=-1.5 * 2.0 ** 23, scale=2.0 ** -12)
+        for lo in range(UB[k], UB[k + 1], 512):
+            s2 = slice(lo, lo + 512)
+            b, b2 = 1 + nb[0] % 3, 4 + nb[0] % 4
+            nb[0] += 1
+            P, P2 = t_["b%d" % b], t_["b%d" % b2]
+            mm([(P[:], t_.ID7[:], t_.ONES[:, 0:512], 512, True, False), (P[:], t_.ID4[:], t_.XX[:, s2], 512, False, True)],
+               ["ID7", "ID4", "ONES", ("XX", k)], b)
+            vtt(t_.D7[:, s2], t_.REC[:, s2], P[:], A.subtract, 512, [("REC", k), ("ps", b)], [("D7", lo)], [b], 1.0)
+            act(t_.A1[:, s2], t_.D7[:, s2], F.Identity, 512, [("D7", lo)], [("A1", lo)], bias=1.5 * 2.0 ** 27)
+            act(t_.HB[:, s2], t_.A1[:, s2], F.Identity, 512, [("A1", lo)], [("HB", lo)], bias=-1.5 * 2.0 ** 27)
+            mm([(P2[:], t_.ID7[:], t_.ONES[:, 0:512], 512, True, False), (P2[:], t_.IDN[:], t_.HB[:, s2], 512, False, False),
+                (P2[:], t_.IDK[:], t_.HB[:, s2], 512, False, True)], ["ID7", "IDN", "IDK", "ONES", ("HB", lo)], b2)
+            vtt(t_.TT[:, s2], t_.D7[:, s2], P2[:], A.add, 512, [("D7", lo), ("ps", b2)], [("TT", k)], [b2], 1.0)
+    vts(t_.THH[:], t_.TH[:], 0.5, None, A.mult, None, 1, ["TH"], ["THH"])
+    vcp(t_.KF[:], t_.MUL[:], 1, ["MUL"], ["KF"])
+    vts(t_.KD[:], t_.IDP[:], t_.KF[:], -1.0, A.mult, A.mult, 128, ["IDP", "KF"], ["KD"], (), 0.5)
+    vts(t_.PR[:], t_.PRI[:], 15, None, A.bitwise_and, None, 16, ["PRI"], ["PR"])
+    vts(t_.ODC[:], t_.PR[:, 0:1], 2.0, 1.0, A.mult, A.add, 1, ["PR"], ["ODC"])
+    vts(t_.OD[:], t_.IDP[:], t_.ODC[:], -1.0, A.mult, A.mult, 128, ["IDP", "ODC"], ["OD"], (), 0.5)
+    vts(t_.R16[:], t_.PR[:], 16.0, None, A.mult, None, 16, ["PR"], ["R16"])
+    vtt(t_.BASE[:], t_.R16[:], t_.I256[:], A.add, 16, ["R16", "I256"], ["BASE"])
+    vtt(t_.DUM[:], t_.PR[:], t_.I16[:], A.add, 16, ["PR", "I16"], ["DUM"])
+    vts(t_.PDC[:], t_.BASE[:], 57344.0, None, A.add, None, 16, ["BASE"], ["PDC"])
+    vts(t_.DMC[:], t_.DUM[:], 57344.0, None, A.add, None, 16, ["DUM"], ["DMC"])
+    vcp(t_.BH[:], t_.BM[:], 128, ["BM"], ["BH"], (), 0.5)
+    vcp(t_.SELH[:], t_.SELB[:], 2048, ["SELB"], ["SELH"], (), 0.5)
+    act(t_.SELM[:], t_.SELB[:], F.Copy, 2048, ["SELB"], ["SELM"], scale=-0.5)
+    vts(t_.H16[:], t_.WT[:], 8.0, 16.0, A.is_ge, A.mult, 256, ["WT"], ["H16"], (), 0.5)
+    vtt(t_.b0[:, 0:256], t_.WT[:], t_.H16[:], A.subtract, 256, ["WT", "H16"], ["W8"], [0])
+
+    TTk = [("TT", k) for k in range(len(UNP))]
+    XXk = [("XX", k) for k in range(len(UNP))]
+    me = T.rank_of(core)
+
+    for t in range(STEPS):
+        last = t == STEPS - 1
+        dst = T.cores[(me + 1 + t % 3) % len(T.cores)]
+        rid, pid, _ = topo.addr(dst)
+        msk, ne = topo.mask(core, dst), len(topo.engines(core, dst))
+        CP, CA, TV, TA, VN, VA = [t_["%s%d" % (x, t)] for x in ("CP", "CA", "TV", "TA", "VN", "VA")]
+
+        def send(m, out, src, R, W_, t=t, rid=rid, pid=pid, msk=msk, ne=ne, after=()):
+            ls, rs = "%s%dl" % (m, t), "%s%dr" % (m, t)
+            add("g", [lambda: g.remote_dma(out, src, T.sem[rs], T.sem[ls], pid, rid, msk)], SND, R, [("sent", m, t)], (), "r",
+                SND, ls, ne, after)
+            add("n", [], ARR, [("sent", m, t)], W_, (), "n", 0.0, rs, ne)
+
+        for lo, hi in C1:
+            m, n = hi - lo, 16 * (hi - lo)
+            es, cs = slice(16 * lo, 16 * hi), slice(lo, hi)
+            add("v", [lambda es=es, cs=cs: g.vector.tensor_tensor(t_.U1[:, es], t_.TT[:, 0:W].indirect(t_.C16[:, cs]),
+                                                                   t_.CKB[:, es], A.subtract)],
+                n * GAM * CYC + 0.05, TTk + ["C16"] + tk("CKB", lo, hi), tk("U1", lo, hi))
+            act(t_.AB[:, es], t_.U1[:, es], F.Abs, n, tk("U1", lo, hi), tk("AB", lo, hi), bias=-4080.0, scale=8192.0)
+            vscan(t_.MN[:, es], t_.MSN[:, 0:n], t_.AB[:, es], A.max, A.min, n, ["MSN"] + tk("AB", lo, hi), tk("MN", lo, hi))
+            vtt(t_.M2[:, cs], t_.MN[:, 16 * lo + 15:16 * hi:16], t_.A32[:, cs], A.min, m, tk("MN", lo, hi) + ["A32"], tk("M2", lo, hi))
+            mm([(t_.b2[:, cs], t_.IDP[:], t_.KM[:, cs], m, True, False), (t_.b2[:, cs], t_.IDN[:], t_.M2[:, cs], m, False, True)],
+               ["IDP", "IDN"] + tk("KM", lo, hi) + tk("M2", lo, hi), 2)
+            vts(CP[:, cs], t_.b2[:, cs], 4080.0, None, A.add, None, m, [("ps", 2)], tk(("CP", t), lo, hi), [2])
+            if not last:
+                mm([(t_.b3[:, cs], t_.IDP[:], t_.KM[:, cs], m, True, False), (t_.b3[:, cs], t_.IDM[:], t_.M2[:, cs], m, False, True)],
+                   ["IDP", "IDM"] + tk("KM", lo, hi) + tk("M2", lo, hi), 3)
+                act(TV[:, cs], t_.b3[:, cs], F.Identity, m, [("ps", 3)], tk(("TV", t), lo, hi), [3], bias=4080.0 / 8192)
+            if hi in SC:
+                l0 = SC[hi]
+                send("e" if hi == 256 else "c", CA[:, l0:hi], CP[:, l0:hi], tk(("CP", t), l0, hi), tk(("CA", t), l0, hi))
+            sgat(t_.XG[:, es], t_.XX[:, 0:W].indirect(CP[:, cs]), n, XXk + tk(("CP", t), lo, hi), tk("XG", lo, hi))
+            vscan(t_.MX[:, es], t_.MSX[:, 0:n], t_.XG[:, es], A.mult, A.max, n, ["MSX"] + tk("XG", lo, hi), tk("MX", lo, hi))
+            vscan(t_.MI[:, es], t_.MSN[:, 0:n], t_.XG[:, es], A.max, A.min, n, ["MSN"] + tk("XG", lo, hi), tk("MI", lo, hi))
+            lc = slice(16 * lo + 15, 16 * hi, 16)
+            mm([(t_.b1[:, cs], t_.IDQ[:], t_.ONES[:, 0:m], m, True, False), (t_.b1[:, cs], t_.IDH[:], t_.MX[:, lc], m, False, False),
+                (t_.b1[:, cs], t_.IDH[:], t_.MI[:, lc], m, False, True)], ["IDQ", "IDH", "ONES"] + tk("MX", lo, hi) + tk("MI", lo, hi), 1)
+            vts(t_.Z[:, cs], t_.b1[:, cs], 1.5 * 2.0 ** 23, -1.5 * 2.0 ** 23, A.add, A.add, m, [("ps", 1)], tk("Z", lo, hi), [1])
+            mm([(t_.b3[:, cs], t_.IDP[:], t_.Z[:, cs], m, True, False), (t_.b3[:, cs], t_.IDN[:], t_.AIM[:, cs], m, False, True)],
+               ["IDP", "IDN", "AIM"] + tk("Z", lo, hi), 3)
+            act(VN[:, cs], t_.b3[:, cs], F.Abs, m, [("ps", 3)], tk(("VN", t), lo, hi), [3])
+            if hi in SV and hi < 256:
+                send("v", VA[:, SV[hi]:hi], VN[:, SV[hi]:hi], tk(("VN", t), SV[hi], hi), tk(("VA", t), SV[hi], hi))
+            vtt(t_.WZ[:, cs], t_.b0[:, cs], t_.Z[:, cs], A.mult, m, ["W8"] + tk("Z", lo, hi), tk("WZ", lo, hi), [0], 1.0)
+            ps = t_.b4[:, 256 + lo // 16:256 + hi // 16]
+            mm([(ps, t_.SELH[:, 128 * r:128 * r + 128], t_.WZ[:, lo + r:hi:16], m // 16, r == 0, r == 15) for r in range(16)],
+               ["SELH"] + tk("WZ", lo, hi), 4)
+        vcp(t_.N32[:], t_.b4[:, 256:272], 16, [("ps", 4)], ["N32"], [4])
+        vts(t_.N15[:], t_.N32[:], 15, None, A.bitwise_and, None, 16, ["N32"], ["N15"])
+        vtt(t_.PI[:], t_.N15[:], t_.BASE[:], A.add, 16, ["N15", "BASE"], ["PI"])
+        vcp(t_.P16[:], t_.PI[:], 16, ["PI"], ["P16"])
+        vscat(t_.XX[:, 0:WP].indirect(t_.P16[:]), VN[:, 0:256], 256, ["P16"] + tk(("VN", t), 0, 256), XXk)
+        vcp(VN[:, 256:272], t_.N15[:], 16, ["N15"], tk(("VN", t), 256, 272))
+        l0 = SV[256]
+        send("w", VA[:, l0:272], VN[:, l0:272], tk(("VN", t), l0, 272), tk(("VA", t), l0, 272))
+        if not last:
+            send("t", TA[:], TV[:], tk(("TV", t), 0, 256), [("TA", t)], after=[len(ops) - 2])
+            vscat(t_.TT[:, 0:WP].indirect(t_.P16[:]), TV[:], 256, ["P16"] + tk(("TV", t), 0, 256), TTk)
+        for hi in SV:
+            l0 = SV[hi]
+            vcp(t_.b0[:, 256 + l0:256 + hi], VA[:, l0:hi], hi - l0, tk(("VA", t), l0, hi), tk("VAP", l0, hi), [0])
+        vtt(t_.PD[:], VA[:, 256:272], t_.PDC[:], A.add, 16, tk(("VA", t), 256, 272) + ["PDC"], ["PD"])
+        if last:
+            dma("y", t_.yz[:], t_.Z[:], 2.5, tk("Z", 0, 256), ["yz"])
+        for c in range(len(C3)):
+            lo, hi = C3[c]
+            n, m = 16 * (hi - lo), hi - lo
+            es, cs = slice(16 * lo, 16 * hi), slice(lo, hi)
+            sgat(t_.XA[:, es], t_.XX[:, 0:W].indirect(CA[:, cs]), n, XXk + tk(("CA", t), lo, hi), tk("XA", lo, hi))
+            bd = 6 + c % 2
+            D = t_["b%d" % bd][:, cs]
+            if c in AC:
+                for h in range(2):
+                    P = t_["b%d" % (2 + h)]
+                    mm([x for j in range(8) for x in
+                        ((P[:, m * j:m * j + m], t_.IDP[:], t_.XA[:, 16 * lo + 8 * h + j:16 * hi:16], m, True, False),
+                         (P[:, m * j:m * j + m], t_.IDN[:], VA[:, cs], m, False, True))],
+                       ["IDP", "IDN"] + tk("XA", lo, hi) + tk(("VA", t), lo, hi), 2 + h)
+                    a0 = 16 * lo + 8 * m * h
+                    act(t_.MXA[:, a0:a0 + 8 * m], P[:, 0:8 * m], F.Abs, 8 * m, [("ps", 2 + h)], [("MXB", lo, h)], [2 + h], scale=0.5)
+                mm([(D, t_.SELB[:, 128 * j:128 * j + 128], t_.MXA[:, 16 * lo + m * j:16 * lo + m * j + m], m, j == 0, j == 15)
+                    for j in range(16)], ["SELB", ("MXB", lo, 0), ("MXB", lo, 1)], bd)
+            else:
+                add("v", [(lambda j=j, lo=lo, hi=hi: g.vector.tensor_tensor(t_.MXA[:, 16 * lo + j:16 * hi:16],
+                           t_.XA[:, 16 * lo + j:16 * hi:16], t_.b0[:, 256 + lo:256 + hi], A.max)) for j in range(16)],
+                    16 * max(64, m) * CYC, tk("XA", lo, hi) + tk("VAP", lo, hi), tk("MXA", lo, hi), [0])
+                mm([(D, t_.BMH[:], VA[:, cs], m, True, False)] +
+                   [(D, t_.SELM[:, 128 * j:128 * j + 128], t_.XA[:, 16 * lo + j:16 * hi:16], m, False, False) for j in range(16)],
+                   ["BMH", "SELM"] + tk(("VA", t), lo, hi) + tk("XA", lo, hi), bd)
+                mm([(D, t_.SELB[:, 128 * j:128 * j + 128], t_.MXA[:, 16 * lo + j:16 * hi:16], m, False, j == 15) for j in range(16)],
+                   ["SELB"] + tk("MXA", lo, hi), bd)
+            vts(t_.FL[:, cs], D, t_.THH[:], 8192.0, A.is_ge, A.mult, m, [("ps", bd), "THH"], tk("FL", lo, hi), [bd])
+            if c not in KG:
+                continue
+            lo = C3[KG[c]][0]
+            m, cs = hi - lo, slice(lo, hi)
+            w = slice(lo // 16, hi // 16)
+            mm([(t_.b1[:, w], t_.SELB[:, 128 * r:128 * r + 128], t_.FL[:, lo + r:hi:16], m // 16, r == 0, r == 15) for r in range(16)],
+               ["SELB"] + tk("FL", lo, hi), 1)
+            vtt(t_.OF[:, w], t_.b1[:, w], t_.PD[:, w], A.max, 4, [("ps", 1), "PD"], [("OF", c)], [1])
+            vtt(t_.OG[:, w], t_.OF[:, w], t_.DMC[:, w], A.min, 4, [("OF", c), "DMC"], [("OG", c)])
+            vts(t_.O16[:, w], t_.OG[:, w], -57344.0, None, A.add, None, 4, [("OG", c)], [("O16", c)])
+            if not last:
+                vscat(t_.TT[:, 0:WP].indirect(t_.O16[:, w]), TA[:, cs], m, [("O16", c), ("TA", t)], TTk)
+        vscat(t_.XX[:, 0:WP].indirect(t_.O16[:]), VA[:, 0:256], 256, [("O16", c) for c in KG] + tk(("VA", t), 0, 256), XXk)
+        Zt, Wt = tk("Z", 0, 256), tk("WZ", 0, 256)
+        vtt(t_.HZ[:], t_.H16[:], t_.Z[:], A.mult, 256, ["H16"] + Zt, ["HZ"])
+        mm([(t_.b4[:, 0:256], t_.BM[:], t_.HZ[:], 256, True, False), (t_.b4[:, 0:256], t_.BH[:], t_.WZ[:], 256, False, True)],
+           ["BM", "BH", "HZ"] + Wt, 4)
+        vcp(t_.UI[:], t_.b4[:, 0:256], 256, [("ps", 4)], ["UI"], [4])
+        vts(t_.UU[:], t_.UI[:], 4095, None, A.bitwise_and, None, 256, ["UI"], ["UU"])
+        vts(t_.UM[:], t_.UU[:], -2048.0, None, A.add, None, 256, ["UU"], ["UM"])
+        vtt(t_.SQ[:], t_.UU[:], t_.UU[:], A.mult, 256, ["UU"], ["SQ"])
+        vts(t_.FF[:], t_.SQ[:], 5, None, A.arith_shift_right, None, 256, ["SQ"], ["FF"])
+        G = t_.b5[:, 0:256]
+        mm([(G, t_.IDN[:], t_.ONES[:, 0:256], 256, True, False), (G, t_.OD[:], t_.Z[:], 256, False, False),
+            (G, t_.KD[:], t_.C2K[:], 256, False, False), (G, t_.KD[:], t_.UM[:], 256, False, True)],
+           ["IDN", "ONES", "OD", "KD", "C2K", "UM"] + Zt, 5)
+        vtt(t_.RP[:], G, t_.FF[:], A.subtract, 256, ["FF", ("ps", 5)], ["RP"], [5], 1.0)
+        if last:
+            vts(t_.CC[:], t_.RP[:], 4095, None, A.bitwise_and, None, 256, ["RP"], ["CC"])
+            vts(t_.YC[:], t_.CC[:], -1.0, 4095.0, A.mult, A.add, 256, ["CC"], ["YC"])
+            dma("y", t_.yc[:], t_.YC[:], 2.5, ["YC"], ["yc"])
+        else:
+            forms()
+            for lo, hi, e in BCN:
+                spread(lo, hi, e)
+    dma("y", t_.yx[:], t_.XX[:, 0:W], 5.0, XXk, ["yx"])
+    return ops, q
+
+
+def rank_program(g, core, T, topo):
+    if T.rank_of(core) is None:
+        return
+    ops, q = build(g, T, core, topo)
+    preds = plan(ops)
+    if "o" not in ORDER:
+        ORDER["o"] = schedule(ops, preds)
+    order = ORDER["o"][0]
+    pos = {}
+    for i in order:
+        pos[i] = len(pos)
+    semof = {"v": "sv", "s": "ss", "t": "st", "g": "sg"}
+    cnt, done, clock, final = {}, {}, {}, {}
+    known = {e: {} for e in q}
+    for i in order:
+        o = ops[i]
+        e = o["e"]
+        if e == "n":
+            done[i] = (o["sem"], o["val"])
+            final[o["sem"]] = o["val"]
+            clock[i] = {}
+            continue
+        kn = known[e]
+        for j in sorted(preds[i], key=lambda x: -pos[x]):
+            if not preds[i][j]:
+                continue
+            s, v = done[j]
+            if kn.get(s, 0) >= v:
+                continue
+            q[e].wait_ge(T.sem[s], v)
+            kn[s] = v
+            for a, b in clock[j].items():
+                if kn.get(a, 0) < b:
+                    kn[a] = b
+        clock[i] = dict(kn)
+        if o["k"] == "c":
+            s = semof[e]
+            for f in o["f"]:
+                f().then_inc(T.sem[s], 1)
+                cnt[s] = cnt.get(s, 0) + 1
+            done[i] = (s, cnt[s])
+        elif o["k"] == "d":
+            o["f"][0]().then_inc(T.sem[o["sem"]], 16)
+            done[i] = (o["sem"], 16)
+        else:
+            o["f"][0]()
+            done[i] = (o["sem"], o["val"])
+        final[done[i][0]] = done[i][1]
+        clock[i][done[i][0]] = done[i][1]
+    for s in sorted(final):
+        if known["g"].get(s, 0) < final[s]:
+            g.wait_ge(T.sem[s], final[s])

@@ -5,23 +5,34 @@ F = ActivationFunctionType
 STEPS = 3
 W = 4096
 WP = W + 256
-C1 = [(0, 64), (64, 128), (128, 192), (192, 256)]
-C3 = [(0, 64), (64, 128), (128, 192), (192, 256)]
+KL, KH = 192, 256
+SP = 192
+C1 = [(0, 64), (64, 128), (128, 192), (192, 224), (224, 256)]
+C1S = [(0, 64), (64, 128), (128, 192), (192, 256)]
+C2 = [(0, 64, "s"), (64, 128, "s"), (128, 192, "s"), (192, 224, "s"), (224, 256, "v")]
+C3 = [(0, 64, "s", 16), (64, 128, "s", 16), (128, 192, "s", 16), (192, 256, "s", 16)]
 SC = {128: 0, 256: 128}
-SV = {128: 0, 256: 128}
-AC = (2,)
-KG = {2: 0, 3: 3}
-BC0 = [(0, 128, "v"), (128, 256, "g")]
-BCN = [(0, 128, "v"), (128, 256, "g")]
-UNP = [512, 512, 1024, 1024, 1024]
-GAM, SCT, CYC, PEC, LAT, WIN = 1.5, 3.5, 0.000833, 0.00042, 0.08, 0.2
-SND, ARR = 1.2, 3.5
-PRI = {"vMXA.12": -1, "vMN.12": -3, "vU1.12": -5, "vWZ.0": -5, "sHB.512": 5, "sHB.3072": 6, "gCKB.8": -11, "sHB.2048": 6,
-       "sA1.3584": 8, "sHB.2560": -1, "vMX.12": -4, "vMI.12": -5, "vTT.4": -6, "tps3.6": 5, "sXX.3": 12, "tps3.14": -7,
-       "sXG.12": -12, "vZ.8": -9, "vZ.4": 4, "vZ.12": -15, "vCP.12": -6, "sVN.0": -10, "tps4.24": 5}
+SV = [(0, 128), (128, 192), (192, 256)]
+CN = [(0, 128), (128, 256)]
+SPR = {128: (0, "gggg"), 192: (128, "gggg")}
+SB = 192
+PU, AU = 256, 1024
+UNP = [512] * 8
+UM = "sdsddsdv"
+CPV = (64, 128, 192, 256)
+CZ = [(0, 64, "t"), (64, 128, "t"), (128, 192, "t"), (192, 256, "v")]
+CV = [(0, 128), (128, 192), (192, 256)]
+ENG = {"FL": "vv", "VAP": "v", "TV": "s", "TA": "s", "TC": "v", "KT": "s", "QQ": "s", "KU": "s"}
+GAM, SCT, CYC, PEC, LAT, LAS, SF = 1.56, 3.8, 0.000833, 0.00044, 0.22, 0.06, 0.1
+SND, ARR = 1.5, 3.5
+ROUNDS, SLACK, SEED = 6000, 0.5, 1
+RUNS = ["vU1.0 vU1.1024 vMN.0 vCP.0 vU1.2048 vMN.1024 vCP.64 vMX.0 vMI.0 vMN.2048 vCP.128 vMX.1024 vMI.1024 vMN.3072 vCP.192",
+        "sA1.3072 sA1.3584 sAB.0 sAB.1024 sXG.0 sAB.2048 sXG.1024 sAB.3072 sXG.2048",
+        "t5HA.0 t7XA.3087 t7MX.3392 t7MX.3776 t7MX.4032", "vMXA.0 vMXA.512 vMXA.1024 vMXA.1536 vMXA.2048 vMXA.2560 vMXA.3072 vMXA.3456 vMXA.3840"]
 ORDER = {}
+M23, M27, M35, M19 = 1.5 * 2.0 ** 23, 1.5 * 2.0 ** 27, 1.5 * 2.0 ** 35, 1.5 * 2.0 ** 19
 
-SCRATCH = {"b%d" % _b: ("psum", [128, 512], "float32") for _b in range(8)}
+SCRATCH = {"b": ("psum", [128, 4096], "float32")}
 
 
 def _sb(cols, dtype, names):
@@ -30,396 +41,594 @@ def _sb(cols, dtype, names):
 
 
 _sb(W, "int32", "REC")
-_sb(W, "float32", "A2 D7 A1")
-_sb(W, "bfloat16", "HB CKB U1 AB MN XG MX MI XA MXA")
+_sb(W, "float32", "A2 A1 CKB")
+_sb(W, "bfloat16", "HT U1 AB MN XG MX MI XA MXA")
 _sb(WP, "float32", "TT")
 _sb(WP, "bfloat16", "XX")
-_sb(256, "int32", "REQ RP CC KK A32 UI UU SQ FF")
-_sb(256, "bfloat16", "AIM WT KM M2 Z H16 HZ FL")
-_sb(256, "float16", "WZ UM C2K")
-_sb(256, "float32", "YC")
+_sb(256, "int32", "REQ RR CC FF")
+_sb(W, "float16", "DC HH")
+_sb(256, "bfloat16", "AIM WT HB HA Z ZO FL QQ KT")
+_sb(256, "float16", "WZ CF HF CG HG")
+_sb(256, "float32", "YC SQ KU TC TV TA CT")
 _sb(256, "uint16", "C16")
 _sb(1, "int32", "MUL TH")
-_sb(1, "float32", "THH KF ODC")
-_sb(2048, "bfloat16", "ONES SELA SELC SELB SELM")
-_sb(2048, "float16", "SELH")
-_sb(128, "bfloat16", "BM0 BM BMH IDP IDN IDK IDM IDH IDQ ID4 ID7 OD")
-_sb(128, "float16", "KD BH")
+_sb(1, "float32", "THH THS KF ODC OB")
+_sb(2048, "bfloat16", "ONES EB")
+_sb(144, "bfloat16", "WS0 WS1 WSB WSM WSG")
+_sb(144, "float16", "WSF")
+_sb(128, "bfloat16", "BM0 BM BMH BMJ BMW IDP IDN IDK IDM IDH IDQ ID2 ID4 ID7 ID8 I7N IBG OD")
+_sb(128, "float16", "IDF BF")
+_sb(128, "float32", "I32")
 _sb(1024, "bfloat16", "MSN MSX")
-_sb(16, "int32", "PRI PR I256 I16 R16 N32 N15")
-_sb(16, "float32", "BASE DUM DMC PDC PI PD OF OG")
+_sb(16, "int32", "PRI PR I256 I16 R16")
+_sb(16, "float32", "BASE BASL DUM DUL FU PI PD OF OG")
 _sb(16, "uint16", "P16 O16")
 for _t in range(STEPS):
     _sb(256, "uint16", "CP%d CA%d" % (_t, _t))
-    _sb(256, "float32", "TV%d TA%d" % (_t, _t))
     _sb(272, "bfloat16", "VN%d VA%d" % (_t, _t))
-SEMAPHORES = ["sv", "ss", "st", "sg"] + ["d%d" % k for k in range(16)] + \
-    ["%s%d%s" % (m, t, x) for m in ("c", "e", "t", "v", "w") for t in range(STEPS) for x in ("l", "r")]
+SEMAPHORES = ["sv", "ss", "st", "sg"] + ["d%d" % k for k in range(24)] + \
+    ["%s%d%s" % (m, t, x) for m in ("c", "e", "u", "v", "w") for t in range(STEPS) for x in ("l", "r")]
 
 
-def tk(name, lo, hi):
-    return [(name, u) for u in range(lo // 16, (hi + 15) // 16)]
+def X(name, lo=0, hi=None, step=1, parts=128):
+    if name[0] == "b":
+        o = 512 * int(name[1])
+        return ("b", o + lo, o + (512 if hi is None else hi), step, parts)
+    return (name, lo, SCRATCH[name][1][1] if hi is None else hi, step, parts)
+
+
+def ind(win, off):
+    return ("@", win, off)
+
+
+def size(a):
+    return (a[2] - a[1] + a[3] - 1) // a[3]
 
 
 def plan(ops):
-    lw, rd, bk = {}, {}, {}
+    hist = {}
     preds = []
     for i in range(len(ops)):
         o = ops[i]
         d = {}
-
-        def need(j, sync):
-            if j != i:
-                d[j] = d.get(j, False) or sync
         for j in o["after"]:
-            need(j, False)
-        for r in o["R"]:
-            if r in lw:
-                need(lw[r], True)
-        for w in o["W"]:
-            if w in lw:
-                need(lw[w], True)
-            for j in rd.get(w, ()):
-                need(j, ops[j]["e"] != o["e"] or ops[j]["k"] != "c")
-        for b in o["B"]:
-            for e, j in bk.get(b, {}).items():
-                need(j, e != o["e"])
-        for r in o["R"]:
-            rd.setdefault(r, []).append(i)
-        for w in o["W"]:
-            lw[w] = i
-            rd[w] = []
-        for b in o["B"]:
-            bk.setdefault(b, {})[o["e"]] = i
+            d[j] = False
+        for acc, wr in [(a, False) for a in o["R"]] + [(a, True) for a in o["W"]]:
+            for lo, hi, j, w, sp in hist.get(acc[0], ()):
+                if sp > 1 and sp == acc[3] and (lo - acc[1]) % sp:
+                    continue
+                if j != i and lo < acc[2] and acc[1] < hi and (w or wr):
+                    sync = w or ops[j]["e"] != o["e"] or ops[j]["k"] != "c"
+                    if w and wr and ops[j]["e"] == "t" and o["e"] == "t":
+                        sync = False
+                    d[j] = d.get(j, False) or sync
+        for a in o["W"]:
+            h = hist.get(a[0], [])
+            if a[3] == 1 and a[4] == 128:
+                h = [x for x in h if not (a[1] <= x[0] and x[1] <= a[2])]
+            elif a[4] == 128:
+                h = [x for x in h if x[:2] != a[1:3] or x[4] != a[3]]
+            hist[a[0]] = h + [(a[1], a[2], i, True, a[3])]
+        for a in o["R"]:
+            hist.setdefault(a[0], []).append((a[1], a[2], i, False, a[3]))
         preds.append(d)
     return preds
 
 
 def schedule(ops, preds):
     n = len(ops)
-    succ = [[] for _ in range(n)]
+    occ, dur, eng, bk = [[o[x] for o in ops] for x in ("occ", "dur", "e", "B")]
+    fw = [[(j, dur[j] + (LAT if eng[i] != eng[j] else LAS) if preds[i][j] else occ[j]) for j in preds[i]] for i in range(n)]
+    bw = [[] for _ in range(n)]
     for i in range(n):
-        for j in preds[i]:
-            succ[j].append(i)
-    bl = [0.0] * n
-    for i in range(n - 1, -1, -1):
-        bl[i] = ops[i]["dur"] + max([bl[j] + LAT for j in succ[i]] + [0.0])
-    bl = [bl[i] + PRI.get(ops[i]["tag"], 0.0) for i in range(n)]
-    cnt = [len(preds[i]) for i in range(n)]
-    rdy = [0.0] * n
-    free = {}
-    avail = [i for i in range(n) if cnt[i] == 0]
-    order, start = [], [0.0] * n
-    end = 0.0
-    while avail:
-        best = None
-        for i in avail:
-            s = max(rdy[i], free.get(ops[i]["e"], 0.0))
-            if best is None or s < best:
-                best, e = s, ops[i]["e"]
-        c = [i for i in avail if ops[i]["e"] == e and max(rdy[i], free.get(e, 0.0)) <= best + WIN]
-        i = max(c, key=lambda x: (bl[x], -x))
-        avail.remove(i)
-        s = max(rdy[i], free.get(e, 0.0))
-        start[i] = s
-        if e != "n":
-            free[e] = s + ops[i]["occ"]
-        f = s + ops[i]["dur"]
-        end = max(end, f)
-        order.append(i)
-        for j in succ[i]:
+        for j, l in fw[i]:
+            bw[j].append((i, occ[i] + l - occ[j]))
+
+    def place(key, lags, run, rel):
+        for i in run:
+            for j, _ in lags[i]:
+                if key[i] <= key[j]:
+                    key[i] = key[j] + 1e-7
+        st = [0.0] * n
+        busy = {e: ([], []) for e in eng}
+        banks = [[] for b in range(8)]
+        for _, i in sorted(zip(key, range(n))):
+            t = rel[i]
+            for j, l in lags[i]:
+                if st[j] + l > t:
+                    t = st[j] + l
+            e, o = eng[i], occ[i]
+            if e != "n":
+                S, E = busy[e]
+                while True:
+                    t0 = t
+                    k = len(E)
+                    while k and E[k - 1] > t + 1e-9:
+                        k -= 1
+                    while k < len(S) and S[k] < t + o - 1e-9:
+                        t = E[k]
+                        k += 1
+                    for b in bk[i]:
+                        for f, s, e2 in banks[b][-12:]:
+                            if f > t and s < t + o and e2 != e:
+                                t = f
+                    if t == t0:
+                        break
+                S.insert(k, t)
+                E.insert(k, t + o)
+                for b in bk[i]:
+                    banks[b].append((t + o + LAT, t - LAT, e))
+            st[i] = t
+        return st
+
+    zero, tail = [0.0] * n, [dur[i] - occ[i] for i in range(n)]
+    cnt = [len(l) for l in fw]
+    run = [i for i in range(n) if cnt[i] == 0]
+    for i in run:
+        for j, _ in bw[i]:
             cnt[j] -= 1
-            rdy[j] = max(rdy[j], f + LAT if preds[j][i] else s)
             if cnt[j] == 0:
-                avail.append(j)
-    return order, start, end
+                run.append(j)
+    assert len(run) == n
+
+    def forward(key):
+        st = place(key, fw, run, zero)
+        return st, max(st[i] + dur[i] for i in range(n))
+
+    def again(st):
+        r = place([-(st[i] + occ[i]) for i in range(n)], bw, run[::-1], tail)
+        return forward([-(r[i] + occ[i]) for i in range(n)])
+
+    bl = [0.0] * n
+    for i in run[::-1]:
+        bl[i] = dur[i] + max([bl[j] + LAT for j, _ in bw[i]] + [0.0])
+    best, end = again(forward([-b for b in bl])[0])
+    cur, cend = best, end
+    seed = [SEED]
+
+    def rnd():
+        seed[0] = (seed[0] * 1103515245 + 12345) % 2147483648
+        return seed[0] / 2147483648.0
+    for it in range(ROUNDS):
+        c, w, a = rnd() * end, 1.0 + 7.0 * rnd(), 4.0 * rnd() ** 2
+        only = "vstg"[int(4 * rnd())] if rnd() < 0.5 else None
+        shake = {ops[i]["tag"]: a * (rnd() - 0.5) for i in range(n) if abs(cur[i] - c) < w and only in (None, eng[i])}
+        every = rnd() < 0.7
+        st, e = forward([cur[i] + (shake.get(ops[i]["tag"], 0.0) if every or abs(cur[i] - c) < w else 0.0) for i in range(n)])
+        if e < cend + 1.0:
+            st, e = again(st)
+        if e <= cend + SLACK * (1.0 - it / ROUNDS) * rnd():
+            cur, cend = st, e
+            if e < end:
+                best, end = st, e
+    order = sorted(range(n), key=lambda x: (best[x], x))
+    extra, user = [[] for _ in range(n)], {}
+    for i in order:
+        for b in bk[i]:
+            extra[i] += [j for e2, j in user.get(b, {}).items() if e2 != eng[i]]
+            user.setdefault(b, {})[eng[i]] = i
+    return order, best, end, extra
 
 
 def build(g, T, core, topo):
     ops = []
     q = {"v": g.vector, "s": g.scalar, "t": g.tensor, "g": g, "y": g.sync}
-    t_ = T
 
-    def add(e, calls, cost, R, W_, B=(), k="c", occ=None, sem=None, val=0, after=()):
-        R, W_ = list(R), list(W_)
-        w0 = W_[0]
-        if isinstance(w0, tuple):
-            u = w0[1]
-            nm = w0[0] if isinstance(w0[0], str) else w0[0][0]
-            if nm == "ps":
-                nm = "ps%d" % u
-                u = len(calls) + (sorted(x[1] for x in R if x[0] in ("M2", "MX", "Z", "WZ", "XA", "MXA", "FL")) + [0])[0]
-            w0 = "%s.%s" % (nm, u)
-        ops.append({"tag": e + w0, "e": e, "f": calls, "dur": cost, "occ": cost if occ is None else occ, "R": R, "W": W_,
-                    "B": list(B), "k": k, "sem": sem, "val": val, "after": list(after)})
+    def ap(a):
+        if not isinstance(a, tuple):
+            return a
+        if a[0] == "@":
+            return ap(a[1]).indirect(ap(a[2]))
+        return T[a[0]][0:a[4], a[1]:a[2]:a[3]] if a[3] > 1 else T[a[0]][0:a[4], a[1]:a[2]]
 
-    def vts(out, i, s1, s2, op0, op1, n, R, W_, B=(), rate=1.0):
+    def parts(l):
+        r = []
+        for a in l:
+            if isinstance(a, tuple):
+                r += [a[1], a[2]] if a[0] == "@" else [a]
+        return r
+
+    def add(e, calls, cost, R, W_, k="c", occ=None, sem=None, val=0, after=()):
+        R = parts(R)
+        nm = W_[0]
+        for a in W_:
+            if a[0] == "@":
+                R.append(a[2])
+                nm = (a[1][0] + a[2][0], a[2][1])
+        W_ = [a[1] if a[0] == "@" else a for a in W_]
+        B = sorted(set(k for a in R + W_ if a[0] == "b" for k in range(a[1] // 512, (a[2] + 511) // 512)))
+        if e == "t":
+            nm = ("%d" % B[0] + R[-1][0][:2], R[-1][1])
+        name = nm[0][:2] if nm[0][:2] in ("CP", "CA", "TV", "TA", "VN", "VA") else nm[0]
+        ops.append({"tag": "%s%s.%s" % (e, name, nm[1]), "e": e, "f": calls, "dur": cost,
+                    "occ": cost if occ is None else occ, "R": R, "W": W_, "B": B, "k": k, "sem": sem, "val": val, "after": list(after)})
+
+    def narrow(*l):
+        return all(SCRATCH[a[0]][2] in ("bfloat16", "float16", "uint16") for a in l)
+
+    def vcost(out, i):
+        if i[0] == "@":
+            return size(out) * GAM * CYC + 0.05
+        if out[0] == "@":
+            return size(i) * SCT * CYC + 0.05
+        return max(64, size(out) * (0.5 if narrow(out, i) else 1.0)) * CYC
+
+    def vts(out, i, s1, s2, op0, op1=None):
         if op1 is None:
-            f = lambda: g.vector.tensor_scalar(out, i, s1, None, op0)
+            f = lambda: g.vector.tensor_scalar(ap(out), ap(i), ap(s1), None, op0)
         else:
-            f = lambda: g.vector.tensor_scalar(out, i, s1, s2, op0, op1)
-        add("v", [f], max(64, n * rate) * CYC, R, W_, B)
+            f = lambda: g.vector.tensor_scalar(ap(out), ap(i), ap(s1), ap(s2), op0, op1)
+        add("v", [f], vcost(out, i), [i, s1, s2], [out])
 
-    def vtt(out, a, b, op, n, R, W_, B=(), rate=2.0):
-        add("v", [lambda: g.vector.tensor_tensor(out, a, b, op)], max(64, n * rate) * CYC, R, W_, B)
+    def vtts(lst, op):
+        c = 0.0
+        for out, a, b in lst:
+            c += vcost(out, a) if a[0] == "@" else max(64, size(out) * (1.0 if "b" in (a[0][0], b[0][0]) else 2.0)) * CYC
+        add("v", [(lambda o=o, a=a, b=b: g.vector.tensor_tensor(ap(o), ap(a), ap(b), op)) for o, a, b in lst], c,
+            [x for o, a, b in lst for x in (a, b)], [o for o, a, b in lst])
 
-    def vcp(out, i, n, R, W_, B=(), rate=1.0):
-        add("v", [lambda: g.vector.tensor_copy(out, i)], max(64, n * rate) * CYC, R, W_, B)
+    def vtt(out, a, b, op):
+        vtts([(out, a, b)], op)
 
-    def vset(ap, c, n, W_):
-        add("v", [lambda: g.vector.memset(ap, c)], max(64, n) * CYC, (), W_)
+    def vcp(out, i):
+        add("v", [lambda: g.vector.tensor_copy(ap(out), ap(i))], vcost(out, i), [i], [out])
 
-    def vscan(out, m, i, op0, op1, n, R, W_):
-        add("v", [lambda: g.vector.tensor_tensor_scan(out, m, i, 0.0, op0, op1)], n * 0.5 * CYC, R, W_)
+    def vset(out, c):
+        add("v", [lambda: g.vector.memset(ap(out), c)], vcost(out, out), (), [out])
 
-    def act(out, i, fn, n, R, W_, B=(), bias=0.0, scale=1.0):
-        add("s", [lambda: g.scalar.activation(out, i, fn, bias=bias, scale=scale)], max(64, n) * CYC + 0.02, R, W_, B)
+    def vscan(out, m, i, op0, op1):
+        add("v", [lambda: g.vector.tensor_tensor_scan(ap(out), ap(m), ap(i), 0.0, op0, op1)], vcost(out, i), [m, i], [out])
 
-    def sgat(out, i, n, R, W_):
-        add("s", [lambda: g.scalar.activation(out, i, F.Copy)], n * GAM * CYC + 0.065, R, W_)
+    def act(out, i, fn, bias=0.0, scale=1.0):
+        c = size(out) * GAM * CYC + 0.065 if i[0] == "@" else size(out) * CYC + SF
+        add("s", [lambda: g.scalar.activation(ap(out), ap(i), fn, bias=ap(bias), scale=ap(scale))], c, [i, bias, scale], [out])
 
-    def vscat(out, i, n, R, W_):
-        add("v", [lambda: g.vector.tensor_copy(out, i)], n * SCT * CYC + 0.05, R, W_)
+    def aff(name, out, i, scale, bias):
+        if ENG[name] == "v":
+            vts(out, i, scale, bias, A.mult, A.add)
+        else:
+            act(out, i, F.Identity, bias=bias, scale=scale)
 
-    def mm(lst, R, b):
-        fs = [(lambda o=o, l=l, r=r, s=s, p=p: g.tensor.matmul(o, l, r, s, p)) for (o, l, r, n, s, p) in lst]
-        add("t", fs, sum(max(64, x[3]) for x in lst) * PEC + 0.03, R, [("ps", b)], [b])
+    tails = {}
+
+    def chain(name):
+        r = [tails[name]] if name in tails else []
+        tails[name] = len(ops)
+        return r
+
+    def gather(e, out, i, after=()):
+        if e == "v":
+            vcp(out, i)
+        else:
+            act(out, i, F.Copy)
+        ops[-1]["after"] = list(after)
+
+    def mm(lst, start=True, stop=True):
+        fs, c = [], 0.03
+        for k in range(len(lst)):
+            o, l, r = lst[k]
+            s = start and (k == 0 or lst[k - 1][0] != o)
+            p = stop and (k == len(lst) - 1 or lst[k + 1][0] != o)
+            fs.append(lambda o=o, l=l, r=r, s=s, p=p: g.tensor.matmul(ap(o), ap(l), ap(r), s, p))
+            c += max(64, size(r)) * PEC * (4 if SCRATCH[r[0]][2] == "float32" else 1)
+        add("t", fs, c, [x for o, l, r in lst for x in (l, r)], [x[0] for x in lst])
 
     nd = [0]
 
     def dma(e, out, i, cost, R, W_):
         s = "d%d" % nd[0]
         nd[0] += 1
-        add(e, [lambda: q[e].dma_start(out, i)], cost, R, W_, (), "d", 0.1, s, 16)
+        add(e, [lambda: q[e].dma_start(out, i)], cost, R, W_, "d", 0.1, s, 16)
 
-    def spread(lo, hi, e):
-        n = hi - lo
-        fs = []
-        for j in range(16):
-            o, i = t_.CKB[:, 16 * lo + j:16 * hi:16], t_.KM[:, lo:hi]
-            if e == "v":
-                fs.append(lambda o=o, i=i: g.vector.tensor_copy(o, i))
-            else:
-                fs.append(lambda o=o, i=i: g.affine_select(o, i, [[0, n]], A.is_equal, 0.0, 0, 0))
-        c = {"v": max(64, n * 0.5) * CYC, "g": 0.17 + 2 * n * CYC}[e]
-        add(e, fs, 16 * c, tk("KM", lo, hi), tk("CKB", lo, hi))
+    def gsel(out, i, pat, op, base, cm):
+        add("g", [lambda: g.affine_select(ap(out), ap(i), pat, op, 0.0, base, cm)], 0.17 + 2 * size(out) * CYC, [i], [out])
+
+    def gio(out, pat, base, cm):
+        add("g", [lambda: g.iota(ap(out), pat, base, cm)], 0.16, (), [out])
+
+    def sel(m, r):
+        return X(m, 15 - r, 143 - r)
 
     UB = [sum(UNP[:k]) for k in range(len(UNP) + 1)]
-    dma("y", t_.REQ[:], t_.req[:], 2.2, (), ["REQ"])
+    dma("y", T.REQ[:], T.req[:], 2.2, (), [X("REQ")])
     for k in range(len(UNP)):
         sl = slice(UB[k], UB[k + 1])
-        dma("s" if k % 2 == 0 else "y", t_.REC[:, sl], t_.rec[:, sl], 2.0 + UB[k + 1] * 0.0016, (), [("REC", k)])
-    dma("y", t_.MUL[:], t_.mul[:], 9.0, (), ["MUL"])
-    dma("y", t_.TH[:], t_.th[:], 9.0, (), ["TH"])
-    dma("s", t_.WT[:], t_.wt[:], 9.0, (), ["WT"])
-    dma("s", t_.AIM[:], t_.aim[:], 9.0, (), ["AIM"])
+        dma("s" if k % 2 == 0 else "y", T.REC[:, sl], T.rec[:, sl], 2.0 + UB[k + 1] * 0.0016, (), [X("REC", UB[k], UB[k + 1])])
+    dma("y", T.MUL[:], T.mul[:], 9.0, (), [X("MUL")])
+    dma("y", T.TH[:], T.th[:], 9.0, (), [X("TH")])
+    dma("s", T.WT[:], T.wt[:], 9.0, (), [X("WT")])
+    dma("s", T.AIM[:], T.aim[:], 9.0, (), [X("AIM")])
 
-    vset(t_.ONES[:], 1.0, 1024, ["ONES"])
-    vset(t_.MSN[:], 0.0, 512, ["MSN"])
-    vset(t_.MSX[:], 1.0, 512, ["MSX"])
-    vset(t_.MSN[:, 0:1024:16], 65536.0, 64, ["MSN"])
-    vset(t_.MSX[:, 0:1024:16], 0.0, 64, ["MSX"])
-    vset(t_.C2K[:], 2048.0, 256, ["C2K"])
+    vset(X("ONES"), 1.0)
+    vset(X("MSN"), 0.0)
+    vset(X("MSX"), 1.0)
+    vset(X("MSN", 0, 1024, 16), 4080.0)
+    vset(X("MSX", 0, 1024, 16), 0.0)
+    vset(X("WS0"), 0.0)
+    vset(X("WS0", 15, 144, 16), 1.0)
+    gsel(X("IDP"), X("ONES", 0, 128), [[-1, 128]], A.is_equal, 0, 1)
+    gio(X("PRI"), [[0, 16]], 0, 1)
+    gio(X("I256"), [[256, 16]], 0, 0)
+    gio(X("I16"), [[16, 16]], W, 0)
+    gsel(X("EB", 0, 16 * (KH - KL)), X("ONES", 0, 16 * (KH - KL)), [[-1, KH - KL], [0, 16]], A.is_equal, 0, 1)
+    gsel(X("BM0"), X("ONES", 0, 128), [[-16, 8], [0, 16]], A.is_ge, 0, 1)
+    gsel(X("BM"), X("BM0"), [[16, 8], [0, 16]], A.is_ge, 15, -1)
+    gsel(X("WS1"), X("WS0"), [[-1, 144]], A.is_ge, 15, 1)
+    gsel(X("WSB"), X("WS1"), [[1, 144]], A.is_ge, 0, -1)
+    for nm, c in (("ID4", 4096.0), ("ID7", 7.5), ("IDN", -1.0), ("IDK", 2.0 ** -14), ("I32", 1.0), ("IDM", -(2.0 ** -14)),
+                  ("IDH", 0.5), ("IDQ", -0.25), ("I7N", -7.5), ("IBG", M19), ("ID2", 2048.0), ("ID8", 8192.0)):
+        act(X(nm), X("IDP"), F.Copy, scale=c)
+    vcp(X("IDF"), X("IDP"))
+    vcp(X("BF"), X("BM"))
+    vcp(X("WSF"), X("WSB"))
+    act(X("BMH"), X("BM"), F.Copy, scale=-0.5)
+    act(X("BMW"), X("BM"), F.Copy, scale=128.0)
+    act(X("WSM"), X("WSB"), F.Copy, scale=-0.5)
+    act(X("WSG"), X("WSB"), F.Copy, scale=16384.0)
+    JS = min([c[3] for c in C3 if c[3]])
+    if JS < 16:
+        gsel(X("BMJ"), X("BMH"), [[0, 8], [-1, 16]], A.is_ge, JS - 1, 0)
 
-    def gsel(out, i, pat, op, base, cm, n, R, W_):
-        add("g", [lambda: g.affine_select(out, i, pat, op, 0.0, base, cm)], 0.17 + 2 * n * CYC, R, W_)
+    def forms(src, lo, hi):
+        vts(X("CF", lo, hi), X(src, lo, hi), -2048.0, None, A.add)
+        vts(X("C16", lo, hi), X("CF", lo, hi), 2048.0, None, A.add)
+        vts(X("HF", lo, hi), X("CF", lo, hi), 2048 + 24576 - 7.5, None, A.add)
+        vts(X("HB", lo, hi), X("HF", lo, hi), -24576.0, None, A.add)
+        for h in SPR:
+            l, e = SPR[h]
+            if not lo < h <= hi:
+                continue
+            P = X("b5", l, h)
+            mm([(P, X("IDF"), X("CF", l, h)), (P, X("IDN"), X("HB", l, h)), (P, X("IDK"), X("HB", l, h))])
+            aff("TC", X("TC", l, h), P, 1.0, 2040.5)
+            o, i = [ap(X("CKB", 16 * l + j, 16 * h, 16)) for j in range(16)], ap(X("TC", l, h))
+            for j in range(0, 16, 4):
+                wr = [X("CKB", 16 * l + k, 16 * h, 16) for k in range(j, j + 4)]
+                if e[j // 4] == "g":
+                    add("g", [(lambda x=x, i=i, n=h - l: g.affine_select(x, i, [[0, n]], A.is_equal, 0.0, 0, 0)) for x in o[j:j + 4]],
+                        4 * (0.17 + 2 * (h - l) * CYC), [X("TC", l, h)], wr)
+                else:
+                    add("s", [(lambda x=x, i=i: g.scalar.activation(x, i, F.Copy)) for x in o[j:j + 4]],
+                        4 * (SF + (h - l) * CYC), [X("TC", l, h)], wr)
+        if lo < KH <= hi:
+            n = KH - KL
+            P, P2 = X("b5", 256, 384, 1, n), X("b5", 384, 512, 1, n)
+            mm([(P, X("CF", KL, KH), X("IDF")), (P, X("HB", KL, KH), X("IDN")), (P2, X("HB", KL, KH), X("IDP"))])
+            aff("KT", X("KT", 0, 128, 1, n), P, -1.0, -2048.0)
+            aff("KT", X("KT", 128, 256, 1, n), P2, -(2.0 ** -14), 0.0)
 
-    def gio(out, pat, base, cm, W_):
-        add("g", [lambda: g.iota(out, pat, base, cm)], 0.16, (), W_)
-    gsel(t_.IDP[:], t_.ONES[:, 0:128], [[-1, 128]], A.is_equal, 0, 1, 128, ["ONES"], ["IDP"])
-    gsel(t_.BM0[:], t_.ONES[:, 0:128], [[-16, 8], [0, 16]], A.is_ge, 0, 1, 128, ["ONES"], ["BM0"])
-    gsel(t_.BM[:], t_.BM0[:], [[16, 8], [0, 16]], A.is_ge, 15, -1, 128, ["BM0"], ["BM"])
-    gio(t_.PRI[:], [[0, 16]], 0, 1, ["PRI"])
-    gio(t_.I256[:], [[256, 16]], 0, 0, ["I256"])
-    gio(t_.I16[:], [[16, 16]], W, 0, ["I16"])
-    gsel(t_.SELA[:], t_.ONES[:], [[1, 16], [0, 8], [-1, 16]], A.is_equal, 0, 0, 2048, ["ONES"], ["SELA"])
-    gsel(t_.SELC[:], t_.SELA[:], [[0, 16], [-16, 8], [0, 16]], A.is_ge, 0, 1, 2048, ["SELA"], ["SELC"])
-    gsel(t_.SELB[:], t_.SELC[:], [[0, 16], [16, 8], [0, 16]], A.is_ge, 15, -1, 2048, ["SELC"], ["SELB"])
-    for nm, c in (("ID4", 4096.0), ("ID7", 7.5), ("IDN", -1.0), ("IDK", 2.0 ** -13), ("IDM", -(2.0 ** -13)), ("IDH", 0.5),
-                  ("IDQ", -0.25)):
-        act(t_[nm][:], t_.IDP[:], F.Copy, 128, ["IDP"], [nm], scale=c)
-    act(t_.BMH[:], t_.BM[:], F.Copy, 128, ["BM"], ["BMH"], scale=-0.5)
+    for lo, hi in CN:
+        forms("REQ", lo, hi)
 
-    def forms():
-        vts(t_.CC[:], t_.RP[:], 4095, None, A.bitwise_and, None, 256, ["RP"], ["CC"])
-        vts(t_.C16[:], t_.CC[:], -1.0, 4095.0, A.mult, A.add, 256, ["CC"], ["C16"])
-        vts(t_.KK[:], t_.RP[:], 15, None, A.bitwise_and, None, 256, ["RP"], ["KK"])
-        vts(t_.KM[:], t_.KK[:], -1.0, 15.0, A.mult, A.add, 256, ["KK"], tk("KM", 0, 256))
-        vts(t_.A32[:], t_.RP[:], 4080, None, A.bitwise_and, None, 256, ["RP"], ["A32"])
-
-    vts(t_.RP[:], t_.REQ[:], -1.0, -1.0, A.mult, A.add, 256, ["REQ"], ["RP"])
-    forms()
-    for lo, hi, e in BC0:
-        spread(lo, hi, e)
-
-    nb = [0]
     for k in range(len(UNP)):
-        sl, n = slice(UB[k], UB[k + 1]), UNP[k]
-        vts(t_.A2[:, sl], t_.REC[:, sl], -2047.5, 1.5 * 2.0 ** 35, A.add, A.add, n, [("REC", k)], [("A2", k)])
-        act(t_.XX[:, sl], t_.A2[:, sl], F.Identity, n, [("A2", k)], [("XX", k)], bias=-1.5 * 2.0 ** 23, scale=2.0 ** -12)
-        for lo in range(UB[k], UB[k + 1], 512):
-            s2 = slice(lo, lo + 512)
-            b, b2 = 1 + nb[0] % 3, 4 + nb[0] % 4
-            nb[0] += 1
-            P, P2 = t_["b%d" % b], t_["b%d" % b2]
-            mm([(P[:], t_.ID7[:], t_.ONES[:, 0:512], 512, True, False), (P[:], t_.ID4[:], t_.XX[:, s2], 512, False, True)],
-               ["ID7", "ID4", "ONES", ("XX", k)], b)
-            vtt(t_.D7[:, s2], t_.REC[:, s2], P[:], A.subtract, 512, [("REC", k), ("ps", b)], [("D7", lo)], [b], 1.0)
-            act(t_.A1[:, s2], t_.D7[:, s2], F.Identity, 512, [("D7", lo)], [("A1", lo)], bias=1.5 * 2.0 ** 27)
-            act(t_.HB[:, s2], t_.A1[:, s2], F.Identity, 512, [("A1", lo)], [("HB", lo)], bias=-1.5 * 2.0 ** 27)
-            mm([(P2[:], t_.ID7[:], t_.ONES[:, 0:512], 512, True, False), (P2[:], t_.IDN[:], t_.HB[:, s2], 512, False, False),
-                (P2[:], t_.IDK[:], t_.HB[:, s2], 512, False, True)], ["ID7", "IDN", "IDK", "ONES", ("HB", lo)], b2)
-            vtt(t_.TT[:, s2], t_.D7[:, s2], P2[:], A.add, 512, [("D7", lo), ("ps", b2)], [("TT", k)], [b2], 1.0)
-    vts(t_.THH[:], t_.TH[:], 0.5, None, A.mult, None, 1, ["TH"], ["THH"])
-    vcp(t_.KF[:], t_.MUL[:], 1, ["MUL"], ["KF"])
-    vts(t_.KD[:], t_.IDP[:], t_.KF[:], -1.0, A.mult, A.mult, 128, ["IDP", "KF"], ["KD"], (), 0.5)
-    vts(t_.PR[:], t_.PRI[:], 15, None, A.bitwise_and, None, 16, ["PRI"], ["PR"])
-    vts(t_.ODC[:], t_.PR[:, 0:1], 2.0, 1.0, A.mult, A.add, 1, ["PR"], ["ODC"])
-    vts(t_.OD[:], t_.IDP[:], t_.ODC[:], -1.0, A.mult, A.mult, 128, ["IDP", "ODC"], ["OD"], (), 0.5)
-    vts(t_.R16[:], t_.PR[:], 16.0, None, A.mult, None, 16, ["PR"], ["R16"])
-    vtt(t_.BASE[:], t_.R16[:], t_.I256[:], A.add, 16, ["R16", "I256"], ["BASE"])
-    vtt(t_.DUM[:], t_.PR[:], t_.I16[:], A.add, 16, ["PR", "I16"], ["DUM"])
-    vts(t_.PDC[:], t_.BASE[:], 57344.0, None, A.add, None, 16, ["BASE"], ["PDC"])
-    vts(t_.DMC[:], t_.DUM[:], 57344.0, None, A.add, None, 16, ["DUM"], ["DMC"])
-    vcp(t_.BH[:], t_.BM[:], 128, ["BM"], ["BH"], (), 0.5)
-    vcp(t_.SELH[:], t_.SELB[:], 2048, ["SELB"], ["SELH"], (), 0.5)
-    act(t_.SELM[:], t_.SELB[:], F.Copy, 2048, ["SELB"], ["SELM"], scale=-0.5)
-    vts(t_.H16[:], t_.WT[:], 8.0, 16.0, A.is_ge, A.mult, 256, ["WT"], ["H16"], (), 0.5)
-    vtt(t_.b0[:, 0:256], t_.WT[:], t_.H16[:], A.subtract, 256, ["WT", "H16"], ["W8"], [0])
+        l0, h0 = UB[k], UB[k + 1]
+        vts(X("A2", l0, h0), X("REC", l0, h0), -2047.5, M35, A.add, A.add)
+        act(X("XX", l0, h0), X("A2", l0, h0), F.Identity, bias=-M23, scale=2.0 ** -12)
+        P, P2 = X(("b1", "b2", "b4")[k % 3]), X(("b3", "b6", "b7")[k % 3])
+        ht = [(P2, X("IDN"), X("HT", l0, h0)), (P2, X("IDK"), X("HT", l0, h0))]
+        if UM[k] == "d":
+            mm([(P, X("ID2"), X("ONES", 0, 512)), (P, X("ID4"), X("XX", l0, h0))])
+            vtt(X("DC", l0, h0), X("REC", l0, h0), P, A.subtract)
+            vts(X("HH", l0, h0), X("DC", l0, h0), 2048 + 24576 - 7.5, None, A.add)
+            vts(X("HT", l0, h0), X("HH", l0, h0), -24576.0, None, A.add)
+            mm([(P2, X("IDF"), X("DC", l0, h0))] + ht)
+            act(X("TT", l0, h0), P2, F.Identity, bias=2040.5)
+            continue
+        mm([(P, X("ID7"), X("ONES", 0, 512)), (P, X("ID4"), X("XX", l0, h0))])
+        vtt(X("A2", l0, h0), X("REC", l0, h0), P, A.subtract)
+        if UM[k] == "s":
+            act(X("A1", l0, h0), X("A2", l0, h0), F.Identity, bias=M27)
+            act(X("HT", l0, h0), X("A1", l0, h0), F.Identity, bias=-M27)
+        else:
+            vts(X("HT", l0, h0), X("A2", l0, h0), M27, -M27, A.add, A.add)
+        mm(ht)
+        vtt(X("TT", l0, h0), X("A2", l0, h0), P2, A.add)
+    vts(X("THH"), X("TH"), 0.5, None, A.mult)
+    vcp(X("KF"), X("MUL"))
+    vts(X("PR"), X("PRI"), 15, None, A.bitwise_and)
+    vts(X("ODC"), X("PR", 0, 1), 2.0, 1.0, A.mult, A.add)
+    vts(X("OB"), X("PR", 0, 1), 256.0, 128.0, A.mult, A.add)
+    vts(X("OD"), X("IDP"), X("ODC"), None, A.mult)
+    vts(X("R16"), X("PR"), 16.0, None, A.mult)
+    vtt(X("PI"), X("R16"), X("I256"), A.add)
+    vts(X("BASE"), X("PI"), 7.5, None, A.add)
+    vtt(X("DUM"), X("PR"), X("I16"), A.add)
+    k = SB // 16
+    vcp(X("BASL", 0, k), X("BASE", 0, k))
+    vcp(X("DUL", 0, k), X("DUM", 0, k))
+    vts(X("BASL", k, 16), X("BASE", k, 16), -16.0 * SB, None, A.add)
+    vts(X("DUL", k, 16), X("DUM", k, 16), -16.0 * SB, None, A.add)
+    vts(X("THS"), X("TH"), -0.5, 0.25, A.mult, A.add)
+    vcp(X("b0", 0, 256), X("WT"))
 
-    TTk = [("TT", k) for k in range(len(UNP))]
-    XXk = [("XX", k) for k in range(len(UNP))]
     me = T.rank_of(core)
-
+    GR = [(0, SP), (SP, 256)]
     for t in range(STEPS):
-        last = t == STEPS - 1
+        last, first = t == STEPS - 1, len(ops)
         dst = T.cores[(me + 1 + t % 3) % len(T.cores)]
         rid, pid, _ = topo.addr(dst)
         msk, ne = topo.mask(core, dst), len(topo.engines(core, dst))
-        CP, CA, TV, TA, VN, VA = [t_["%s%d" % (x, t)] for x in ("CP", "CA", "TV", "TA", "VN", "VA")]
+        CP, CA, VN, VA = ["%s%d" % (x, t) for x in ("CP", "CA", "VN", "VA")]
 
-        def send(m, out, src, R, W_, t=t, rid=rid, pid=pid, msk=msk, ne=ne, after=()):
+        def send(m, out, src, t=t, rid=rid, pid=pid, msk=msk, ne=ne):
             ls, rs = "%s%dl" % (m, t), "%s%dr" % (m, t)
-            add("g", [lambda: g.remote_dma(out, src, T.sem[rs], T.sem[ls], pid, rid, msk)], SND, R, [("sent", m, t)], (), "r",
-                SND, ls, ne, after)
-            add("n", [], ARR, [("sent", m, t)], W_, (), "n", 0.0, rs, ne)
+            tok = ("sent" + ls, 0, 1, 1, 128)
+            add("g", [lambda: g.remote_dma(ap(out), ap(src), T.sem[rs], T.sem[ls], pid, rid, msk)], SND, [src], [tok], "r", SND, ls, ne,
+                chain("send"))
+            ops[-1]["tag"] = "gsend." + m
+            add("n", [], ARR, [tok], [out], "n", 0.0, rs, ne)
 
         for lo, hi in C1:
-            m, n = hi - lo, 16 * (hi - lo)
-            es, cs = slice(16 * lo, 16 * hi), slice(lo, hi)
-            add("v", [lambda es=es, cs=cs: g.vector.tensor_tensor(t_.U1[:, es], t_.TT[:, 0:W].indirect(t_.C16[:, cs]),
-                                                                   t_.CKB[:, es], A.subtract)],
-                n * GAM * CYC + 0.05, TTk + ["C16"] + tk("CKB", lo, hi), tk("U1", lo, hi))
-            act(t_.AB[:, es], t_.U1[:, es], F.Abs, n, tk("U1", lo, hi), tk("AB", lo, hi), bias=-4080.0, scale=8192.0)
-            vscan(t_.MN[:, es], t_.MSN[:, 0:n], t_.AB[:, es], A.max, A.min, n, ["MSN"] + tk("AB", lo, hi), tk("MN", lo, hi))
-            vtt(t_.M2[:, cs], t_.MN[:, 16 * lo + 15:16 * hi:16], t_.A32[:, cs], A.min, m, tk("MN", lo, hi) + ["A32"], tk("M2", lo, hi))
-            mm([(t_.b2[:, cs], t_.IDP[:], t_.KM[:, cs], m, True, False), (t_.b2[:, cs], t_.IDN[:], t_.M2[:, cs], m, False, True)],
-               ["IDP", "IDN"] + tk("KM", lo, hi) + tk("M2", lo, hi), 2)
-            vts(CP[:, cs], t_.b2[:, cs], 4080.0, None, A.add, None, m, [("ps", 2)], tk(("CP", t), lo, hi), [2])
-            if not last:
-                mm([(t_.b3[:, cs], t_.IDP[:], t_.KM[:, cs], m, True, False), (t_.b3[:, cs], t_.IDM[:], t_.M2[:, cs], m, False, True)],
-                   ["IDP", "IDM"] + tk("KM", lo, hi) + tk("M2", lo, hi), 3)
-                act(TV[:, cs], t_.b3[:, cs], F.Identity, m, [("ps", 3)], tk(("TV", t), lo, hi), [3], bias=4080.0 / 8192)
-            if hi in SC:
-                l0 = SC[hi]
-                send("e" if hi == 256 else "c", CA[:, l0:hi], CP[:, l0:hi], tk(("CP", t), l0, hi), tk(("CA", t), l0, hi))
-            sgat(t_.XG[:, es], t_.XX[:, 0:W].indirect(CP[:, cs]), n, XXk + tk(("CP", t), lo, hi), tk("XG", lo, hi))
-            vscan(t_.MX[:, es], t_.MSX[:, 0:n], t_.XG[:, es], A.mult, A.max, n, ["MSX"] + tk("XG", lo, hi), tk("MX", lo, hi))
-            vscan(t_.MI[:, es], t_.MSN[:, 0:n], t_.XG[:, es], A.max, A.min, n, ["MSN"] + tk("XG", lo, hi), tk("MI", lo, hi))
-            lc = slice(16 * lo + 15, 16 * hi, 16)
-            mm([(t_.b1[:, cs], t_.IDQ[:], t_.ONES[:, 0:m], m, True, False), (t_.b1[:, cs], t_.IDH[:], t_.MX[:, lc], m, False, False),
-                (t_.b1[:, cs], t_.IDH[:], t_.MI[:, lc], m, False, True)], ["IDQ", "IDH", "ONES"] + tk("MX", lo, hi) + tk("MI", lo, hi), 1)
-            vts(t_.Z[:, cs], t_.b1[:, cs], 1.5 * 2.0 ** 23, -1.5 * 2.0 ** 23, A.add, A.add, m, [("ps", 1)], tk("Z", lo, hi), [1])
-            mm([(t_.b3[:, cs], t_.IDP[:], t_.Z[:, cs], m, True, False), (t_.b3[:, cs], t_.IDN[:], t_.AIM[:, cs], m, False, True)],
-               ["IDP", "IDN", "AIM"] + tk("Z", lo, hi), 3)
-            act(VN[:, cs], t_.b3[:, cs], F.Abs, m, [("ps", 3)], tk(("VN", t), lo, hi), [3])
-            if hi in SV and hi < 256:
-                send("v", VA[:, SV[hi]:hi], VN[:, SV[hi]:hi], tk(("VN", t), SV[hi], hi), tk(("VA", t), SV[hi], hi))
-            vtt(t_.WZ[:, cs], t_.b0[:, cs], t_.Z[:, cs], A.mult, m, ["W8"] + tk("Z", lo, hi), tk("WZ", lo, hi), [0], 1.0)
-            ps = t_.b4[:, 256 + lo // 16:256 + hi // 16]
-            mm([(ps, t_.SELH[:, 128 * r:128 * r + 128], t_.WZ[:, lo + r:hi:16], m // 16, r == 0, r == 15) for r in range(16)],
-               ["SELH"] + tk("WZ", lo, hi), 4)
-        vcp(t_.N32[:], t_.b4[:, 256:272], 16, [("ps", 4)], ["N32"], [4])
-        vts(t_.N15[:], t_.N32[:], 15, None, A.bitwise_and, None, 16, ["N32"], ["N15"])
-        vtt(t_.PI[:], t_.N15[:], t_.BASE[:], A.add, 16, ["N15", "BASE"], ["PI"])
-        vcp(t_.P16[:], t_.PI[:], 16, ["PI"], ["P16"])
-        vscat(t_.XX[:, 0:WP].indirect(t_.P16[:]), VN[:, 0:256], 256, ["P16"] + tk(("VN", t), 0, 256), XXk)
-        vcp(VN[:, 256:272], t_.N15[:], 16, ["N15"], tk(("VN", t), 256, 272))
-        l0 = SV[256]
-        send("w", VA[:, l0:272], VN[:, l0:272], tk(("VN", t), l0, 272), tk(("VA", t), l0, 272))
-        if not last:
-            send("t", TA[:], TV[:], tk(("TV", t), 0, 256), [("TA", t)], after=[len(ops) - 2])
-            vscat(t_.TT[:, 0:WP].indirect(t_.P16[:]), TV[:], 256, ["P16"] + tk(("TV", t), 0, 256), TTk)
-        for hi in SV:
-            l0 = SV[hi]
-            vcp(t_.b0[:, 256 + l0:256 + hi], VA[:, l0:hi], hi - l0, tk(("VA", t), l0, hi), tk("VAP", l0, hi), [0])
-        vtt(t_.PD[:], VA[:, 256:272], t_.PDC[:], A.add, 16, tk(("VA", t), 256, 272) + ["PDC"], ["PD"])
-        if last:
-            dma("y", t_.yz[:], t_.Z[:], 2.5, tk("Z", 0, 256), ["yz"])
-        for c in range(len(C3)):
-            lo, hi = C3[c]
-            n, m = 16 * (hi - lo), hi - lo
-            es, cs = slice(16 * lo, 16 * hi), slice(lo, hi)
-            sgat(t_.XA[:, es], t_.XX[:, 0:W].indirect(CA[:, cs]), n, XXk + tk(("CA", t), lo, hi), tk("XA", lo, hi))
-            bd = 6 + c % 2
-            D = t_["b%d" % bd][:, cs]
-            if c in AC:
-                for h in range(2):
-                    P = t_["b%d" % (2 + h)]
-                    mm([x for j in range(8) for x in
-                        ((P[:, m * j:m * j + m], t_.IDP[:], t_.XA[:, 16 * lo + 8 * h + j:16 * hi:16], m, True, False),
-                         (P[:, m * j:m * j + m], t_.IDN[:], VA[:, cs], m, False, True))],
-                       ["IDP", "IDN"] + tk("XA", lo, hi) + tk(("VA", t), lo, hi), 2 + h)
-                    a0 = 16 * lo + 8 * m * h
-                    act(t_.MXA[:, a0:a0 + 8 * m], P[:, 0:8 * m], F.Abs, 8 * m, [("ps", 2 + h)], [("MXB", lo, h)], [2 + h], scale=0.5)
-                mm([(D, t_.SELB[:, 128 * j:128 * j + 128], t_.MXA[:, 16 * lo + m * j:16 * lo + m * j + m], m, j == 0, j == 15)
-                    for j in range(16)], ["SELB", ("MXB", lo, 0), ("MXB", lo, 1)], bd)
+            el, eh = 16 * lo, 16 * hi
+            names = ind(X("TT", 0, W), X("C16", lo, hi))
+            if not KL <= lo < KH:
+                vtt(X("U1", el, eh), names, X("CKB", el, eh), A.subtract)
+                act(X("AB", el, eh), X("U1", el, eh), F.Abs, bias=4080.0, scale=-16384.0)
             else:
-                add("v", [(lambda j=j, lo=lo, hi=hi: g.vector.tensor_tensor(t_.MXA[:, 16 * lo + j:16 * hi:16],
-                           t_.XA[:, 16 * lo + j:16 * hi:16], t_.b0[:, 256 + lo:256 + hi], A.max)) for j in range(16)],
-                    16 * max(64, m) * CYC, tk("XA", lo, hi) + tk("VAP", lo, hi), tk("MXA", lo, hi), [0])
-                mm([(D, t_.BMH[:], VA[:, cs], m, True, False)] +
-                   [(D, t_.SELM[:, 128 * j:128 * j + 128], t_.XA[:, 16 * lo + j:16 * hi:16], m, False, False) for j in range(16)],
-                   ["BMH", "SELM"] + tk(("VA", t), lo, hi) + tk("XA", lo, hi), bd)
-                mm([(D, t_.SELB[:, 128 * j:128 * j + 128], t_.MXA[:, 16 * lo + j:16 * hi:16], m, False, j == 15) for j in range(16)],
-                   ["SELB"] + tk("MXA", lo, hi), bd)
-            vts(t_.FL[:, cs], D, t_.THH[:], 8192.0, A.is_ge, A.mult, m, [("ps", bd), "THH"], tk("FL", lo, hi), [bd])
-            if c not in KG:
+                gather("s", X("A1", el, eh), names)
+        for l0 in range(16 * KL, 16 * KH, AU):
+            o = (l0 - 16 * KL) % 1024
+            for l in range(l0, l0 + AU, PU):
+                P = X("b1", o + l - l0, o + l - l0 + PU)
+                e = X("EB", l - 16 * KL, l + PU - 16 * KL, 1, KH - KL)
+                mm([(P, X("KT", 0, 128, 1, KH - KL), e), (P, X("KT", 128, 256, 1, KH - KL), e), (P, X("I32"), X("A1", l, l + PU))])
+            act(X("AB", l0, l0 + AU), X("b1", o, o + AU), F.Abs, bias=4080.0 - 7.5 * 16384, scale=-16384.0)
+        for lo, hi in C1S:
+            n = 16 * (hi - lo)
+            el, eh = 16 * lo, 16 * hi
+            vscan(X("MN", el, eh), X("MSN", 0, n), X("AB", el, eh), A.max, A.min)
+            mn = X("MN", el + 15, eh, 16)
+            if hi in CPV:
+                vtt(X("CT", lo, hi), X("CF", lo, hi), mn, A.subtract)
+                vts(X(CP, lo, hi), X("CT", lo, hi), 2048.0 + 4080.0, None, A.add)
+            else:
+                P = X("b3", lo, hi)
+                mm([(P, X("IDF"), X("CF", lo, hi)), (P, X("IDN"), mn)])
+                vts(X(CP, lo, hi), P, 2048.0 + 4080.0, None, A.add)
+            if hi in SC:
+                send("e" if hi == 256 else "c", X(CA, SC[hi], hi), X(CP, SC[hi], hi))
+        if not last:
+            P = X("b4", 0, 256)
+            mm([(P, X("IDF"), X("CF")), (P, X("IDN"), X("HB")), (P, X("IDK"), X("HB"))], True, False)
+            mm([(P, X("IDM"), X("MN", 15, W, 16))], False, True)
+            aff("TV", X("TV"), P, 1.0, 2040.5 + 4080.0 / 16384)
+        for lo, hi, e in C2:
+            n = 16 * (hi - lo)
+            el, eh = 16 * lo, 16 * hi
+            gather(e, X("XG", el, eh), ind(X("XX", 0, W), X(CP, lo, hi)), chain("x" + e))
+            vscan(X("MX", el, eh), X("MSX", 0, n), X("XG", el, eh), A.mult, A.max)
+            vscan(X("MI", el, eh), X("MSN", 0, n), X("XG", el, eh), A.max, A.min)
+        for lo, hi, e in CZ:
+            el, eh = 16 * lo, 16 * hi
+            if e == "v":
+                vtt(X("CT", lo, hi), X("MX", el + 15, eh, 16), X("MI", el + 15, eh, 16), A.add)
+                vts(X("FF", lo, hi), X("CT", lo, hi), 0.5, -128.25, A.mult, A.add)
+                vtt(X("WZ", lo, hi), X("FF", lo, hi), X("b0", lo, hi), A.mult)
+                vcp(X("Z", lo, hi), X("FF", lo, hi))
                 continue
-            lo = C3[KG[c]][0]
-            m, cs = hi - lo, slice(lo, hi)
-            w = slice(lo // 16, hi // 16)
-            mm([(t_.b1[:, w], t_.SELB[:, 128 * r:128 * r + 128], t_.FL[:, lo + r:hi:16], m // 16, r == 0, r == 15) for r in range(16)],
-               ["SELB"] + tk("FL", lo, hi), 1)
-            vtt(t_.OF[:, w], t_.b1[:, w], t_.PD[:, w], A.max, 4, [("ps", 1), "PD"], [("OF", c)], [1])
-            vtt(t_.OG[:, w], t_.OF[:, w], t_.DMC[:, w], A.min, 4, [("OF", c), "DMC"], [("OG", c)])
-            vts(t_.O16[:, w], t_.OG[:, w], -57344.0, None, A.add, None, 4, [("OG", c)], [("O16", c)])
+            P = X("b3", 256 + lo, 256 + hi)
+            mm([(P, X("IDQ"), X("ONES", 0, hi - lo)), (P, X("IDH"), X("MX", el + 15, eh, 16)), (P, X("IDH"), X("MI", el + 15, eh, 16))])
+            vts(X("Z", lo, hi), P, M23, -M23 - 128, A.add, A.add)
+            vtt(X("WZ", lo, hi), X("Z", lo, hi), X("b0", lo, hi), A.mult)
+        for lo, hi in CV:
+            P = X("b2", lo, hi)
+            mm([(P, X("IDN"), X("AIM", lo, hi)), (P, X("IDP"), X("Z", lo, hi))])
+            act(X(VN, lo, hi), P, F.Abs, bias=128.0)
+        for lo, hi in GR:
+            wl, wh = lo // 16, hi // 16
+            P = X("b7", 480 + wl, 480 + wh)
+            mm([(P, X("I7N"), X("ONES", 0, wh - wl))] + [(P, sel("WSF", r), X("WZ", lo + r, hi, 16)) for r in range(16)])
+            vts(X("FU", wl, wh), P, M27, -M27, A.add, A.add)
+            nn = X(VN, 256 + wl, 256 + wh)
+            vtt(nn, P, X("FU", wl, wh), A.subtract)
+            if lo == 0:
+                vtt(X("PI", wl, wh), nn, X("BASE", wl, wh), A.add)
+                vcp(X("P16", wl, wh), X("PI", wl, wh))
+            else:
+                for w in range(wl, wh):
+                    vts(X("P16", w, w + 1), X("b7", 480 + w, 481 + w), X("FU", w, w + 1), X("BASE", w, w + 1), A.subtract, A.add)
+        for k in range(len(SV)):
+            lo, hi = SV[k]
+            hi += 16 if hi == 256 else 0
+            send("uvw"[k - len(SV)], X(VA, lo, hi), X(VN, lo, hi))
+        for lo, hi in GR:
+            vcp(ind(X("XX", 0, W), X("P16", lo // 16, hi // 16)), X(VN, lo, hi))
             if not last:
-                vscat(t_.TT[:, 0:WP].indirect(t_.O16[:, w]), TA[:, cs], m, [("O16", c), ("TA", t)], TTk)
-        vscat(t_.XX[:, 0:WP].indirect(t_.O16[:]), VA[:, 0:256], 256, [("O16", c) for c in KG] + tk(("VA", t), 0, 256), XXk)
-        Zt, Wt = tk("Z", 0, 256), tk("WZ", 0, 256)
-        vtt(t_.HZ[:], t_.H16[:], t_.Z[:], A.mult, 256, ["H16"] + Zt, ["HZ"])
-        mm([(t_.b4[:, 0:256], t_.BM[:], t_.HZ[:], 256, True, False), (t_.b4[:, 0:256], t_.BH[:], t_.WZ[:], 256, False, True)],
-           ["BM", "BH", "HZ"] + Wt, 4)
-        vcp(t_.UI[:], t_.b4[:, 0:256], 256, [("ps", 4)], ["UI"], [4])
-        vts(t_.UU[:], t_.UI[:], 4095, None, A.bitwise_and, None, 256, ["UI"], ["UU"])
-        vts(t_.UM[:], t_.UU[:], -2048.0, None, A.add, None, 256, ["UU"], ["UM"])
-        vtt(t_.SQ[:], t_.UU[:], t_.UU[:], A.mult, 256, ["UU"], ["SQ"])
-        vts(t_.FF[:], t_.SQ[:], 5, None, A.arith_shift_right, None, 256, ["SQ"], ["FF"])
-        G = t_.b5[:, 0:256]
-        mm([(G, t_.IDN[:], t_.ONES[:, 0:256], 256, True, False), (G, t_.OD[:], t_.Z[:], 256, False, False),
-            (G, t_.KD[:], t_.C2K[:], 256, False, False), (G, t_.KD[:], t_.UM[:], 256, False, True)],
-           ["IDN", "ONES", "OD", "KD", "C2K", "UM"] + Zt, 5)
-        vtt(t_.RP[:], G, t_.FF[:], A.subtract, 256, ["FF", ("ps", 5)], ["RP"], [5], 1.0)
+                vcp(ind(X("TT", 0, W), X("P16", lo // 16, hi // 16)), X("TV", lo, hi))
         if last:
-            vts(t_.CC[:], t_.RP[:], 4095, None, A.bitwise_and, None, 256, ["RP"], ["CC"])
-            vts(t_.YC[:], t_.CC[:], -1.0, 4095.0, A.mult, A.add, 256, ["CC"], ["YC"])
-            dma("y", t_.yc[:], t_.YC[:], 2.5, ["YC"], ["yc"])
-        else:
-            forms()
-            for lo, hi, e in BCN:
-                spread(lo, hi, e)
-    dma("y", t_.yx[:], t_.XX[:, 0:W], 5.0, XXk, ["yx"])
+            vts(X("ZO"), X("Z"), 128.0, None, A.add)
+            dma("y", T.yz[:], T.ZO[:], 2.5, [X("ZO")], [("yz", 0, 1, 1, 128)])
+        for lo, hi in CN:
+            wz, wt = X("WZ", lo, hi), X("WT", lo, hi)
+            P = X("b5", lo, hi)
+            mm([(P, X("BF"), wz), (P, X("BMW"), wt)])
+            aff("QQ", X("QQ", lo, hi), P, 1.0, M19 - 2047.5)
+            P = X("b5", 256 + lo, 256 + hi)
+            mm([(P, X("IBG"), X("ONES", 0, hi - lo)), (P, X("IDN"), X("QQ", lo, hi)), (P, X("BF"), wz), (P, X("BMW"), wt)])
+            act(X("SQ", lo, hi), P, F.Square)
+            aff("KU", X("KU", lo, hi), P, X("KF"), X("OB"))
+            vts(X("FF", lo, hi), X("SQ", lo, hi), 1.0 / 32, -0.375, A.mult, A.add)
+            P = X("b3", lo, hi)
+            mm([(P, X("I32"), X("KU", lo, hi)), (P, X("OD"), X("Z", lo, hi))])
+            vtt(X("RR", lo, hi), X("FF", lo, hi), P, A.add)
+            vts(X("CC", lo, hi), X("RR", lo, hi), 4095, None, A.bitwise_and)
+            if last:
+                vcp(X("YC", lo, hi), X("CC", lo, hi))
+            else:
+                forms("CC", lo, hi)
+        if last:
+            dma("y", T.yc[:], T.YC[:], 2.5, [X("YC")], [("yc", 0, 1, 1, 128)])
+        if not last:
+            vts(X("CG"), X(CA), -2048.0, None, A.add)
+            vts(X("HG"), X("CG"), 2048 + 24576 - 7.5, None, A.add)
+            vts(X("HA"), X("HG"), -24576.0, None, A.add)
+            P = X("b5", 0, 256)
+            mm([(P, X("IDF"), X("CG")), (P, X("IDN"), X("HA")), (P, X("IDK"), X("HA"))])
+            aff("TA", X("TA"), P, 1.0, 2040.5)
+        for lo, hi in SV:
+            hi = max([lo] + [c[1] for c in C3 if c[1] - c[0] > 32 and c[3] and c[1] <= hi])
+            if hi == lo:
+                continue
+            if ENG["VAP"] == "v":
+                vcp(X("b0", 256 + lo, 256 + hi), X(VA, lo, hi))
+            else:
+                act(X("b0", 256 + lo, 256 + hi), X(VA, lo, hi), F.Copy)
+        vtt(X("PD"), X(VA, 256, 272), X("BASL" if last else "BASE"), A.add)
+        for c in range(len(C3)):
+            lo, hi, e, js = C3[c]
+            m = hi - lo
+            el, eh = 16 * lo, 16 * hi
+            va = X(VA, lo, hi)
+            gather(e, X("XA", el, eh), ind(X("XX", 0, W), X(CA, lo, hi)), chain("x" + e))
+            D = X("b%d" % (6, 4, 2, 7, 6)[c], 0, m)
+            xa = [X("XA", el + j, eh, 16) for j in range(16)]
+            mx = [X("MXA", el + m * j, el + m * j + m) for j in range(16)]
+            if js:
+                mm([(D, sel("WSM", j), xa[j]) for j in range(js)], True, False)
+            runs = ([(0, js // 2), (js // 2, js)] if hi < 256 else [(0, 6), (6, 12), (12, 16)]) + [(j, min(j + 512 // m, 16)) for j in range(js, 16, 512 // m)]
+            for j0, j1 in runs:
+                if j1 == j0:
+                    continue
+                if j1 <= js:
+                    vtts([(mx[j], xa[j], va if m <= 32 else X("b0", 256 + lo, 256 + hi)) for j in range(j0, j1)], A.max)
+                else:
+                    b = "b1"
+                    mm([x for j in range(j0, j1) for x in ((X(b, m * (j - j0), m * (j - j0 + 1)), X("IDP"), xa[j]),
+                                                           (X(b, m * (j - j0), m * (j - j0 + 1)), X("IDN"), va))])
+                    act(X("MXA", el + m * j0, el + m * j1), X(b, 0, m * (j1 - j0)), F.Abs, scale=0.5)
+                mm([(D, X("BMH" if js == 16 else "BMJ"), va)] * (j0 == 0 and js > 0) +
+                   [(D, sel("WSB", j), mx[j]) for j in range(j0, j1)], j0 == 0 and js == 0, j1 == 16)
+            fe = ENG["FL"][0 if hi <= SB else 1]
+            if fe == "v":
+                vts(X("FL", lo, hi), D, X("THH"), -15.0 / 32, A.is_ge, A.add)
+            else:
+                act(X("FL", lo, hi), D, F.Sign, bias=X("THS"))
+            if hi not in (SB, 256):
+                continue
+            lo = 0 if hi == SB else SB
+            wl, wh = lo // 16, hi // 16
+            P = X("b3", 480 + wl, 480 + wh)
+            mm([(P, X("ID8"), X("ONES", 0, wh - wl))] * (fe == "s") + [(P, sel("WSG", r), X("FL", lo + r, hi, 16)) for r in range(16)])
+            dum = "DUL" if last else "DUM"
+            if lo == 0:
+                vtt(X("OF", wl, wh), P, X("PD", wl, wh), A.max)
+                vtt(X("OG", wl, wh), X("OF", wl, wh), X(dum, wl, wh), A.min)
+                vcp(X("O16", wl, wh), X("OG", wl, wh))
+            else:
+                for w in range(wl, wh):
+                    vts(X("O16", w, w + 1), X("b3", 480 + w, 481 + w), X("PD", w, w + 1), X(dum, w, w + 1), A.max, A.min)
+            if not last:
+                vcp(ind(X("TT"), X("O16", wl, wh)), X("TA", lo, hi))
+        for lo, hi in ((0, SB), (SB, 256)):
+            vcp(ind(X("XX", 16 * lo if last else 0, WP), X("O16", lo // 16, hi // 16)), X(VA, lo, hi))
+            if last:
+                dma("y" if lo == 0 else "s", T.yx[:, 16 * lo:16 * hi], T.XX[:, 16 * lo:16 * hi], 2.0 + (hi - lo) * 0.012,
+                    [X("XX", 16 * lo, 16 * hi)], [("yx%d" % lo, 0, 1, 1, 128)])
+        at = {ops[i]["tag"]: i for i in range(first, len(ops))}
+        for run in RUNS:
+            run = [at[x] for x in run.split() if x in at]
+            for a, b in zip(run, run[1:]):
+                ops[b]["after"].append(a)
     return ops, q
 
 
@@ -427,10 +636,14 @@ def rank_program(g, core, T, topo):
     if T.rank_of(core) is None:
         return
     ops, q = build(g, T, core, topo)
-    preds = plan(ops)
     if "o" not in ORDER:
-        ORDER["o"] = schedule(ops, preds)
-    order = ORDER["o"][0]
+        preds = plan(ops)
+        order, start, end, extra = schedule(ops, preds)
+        for i in range(len(ops)):
+            for j in extra[i]:
+                preds[i][j] = True
+        ORDER["o"] = (order, preds)
+    order, preds = ORDER["o"]
     pos = {}
     for i in order:
         pos[i] = len(pos)

@@ -1,3 +1,4 @@
+import math
 from concourse.mybir import dt, AluOpType, AxisListType, ActivationFunctionType
 
 A = AluOpType
@@ -9,26 +10,27 @@ KL, KH = 192, 256
 SP = 192
 C1 = [(0, 64), (64, 128), (128, 192), (192, 224), (224, 256)]
 C1S = [(0, 64), (64, 128), (128, 192), (192, 256)]
-C2 = [(0, 64, "s"), (64, 128, "s"), (128, 192, "s"), (192, 224, "s"), (224, 256, "v")]
+C2 = [(0, 32, "v"), (32, 64, "s"), (64, 128, "s"), (128, 192, "s"), (192, 224, "s"), (224, 256, "s")]
 C3 = [(0, 64, "s", 16), (64, 128, "s", 16), (128, 192, "s", 16), (192, 256, "s", 16)]
 SC = {128: 0, 256: 128}
 SV = [(0, 128), (128, 192), (192, 256)]
-CN = [(0, 128), (128, 256)]
-SPR = {128: (0, "gggg"), 192: (128, "gggg")}
+CN = [(0, 192), (192, 256)]
+SPR = {192: (0, "ggss")}
 SB = 192
-PU, AU = 256, 1024
+PU, AU = 256, 512
 UNP = [512] * 8
 UM = "sdsddsdv"
-CPV = (64, 128, 192, 256)
-CZ = [(0, 64, "t"), (64, 128, "t"), (128, 192, "t"), (192, 256, "v")]
+CPV = ()
+CZ = [(0, 64, "t"), (64, 128, "t"), (128, 192, "t"), (192, 256, "t")]
 CV = [(0, 128), (128, 192), (192, 256)]
-ENG = {"FL": "vv", "VAP": "v", "TV": "s", "TA": "s", "TC": "v", "KT": "s", "QQ": "s", "KU": "s"}
-GAM, SCT, CYC, PEC, LAT, LAS, SF = 1.56, 3.8, 0.000833, 0.00044, 0.22, 0.06, 0.1
-SND, ARR = 1.5, 3.5
-ROUNDS, SLACK, SEED = 6000, 0.5, 1
-RUNS = ["vU1.0 vU1.1024 vMN.0 vCP.0 vU1.2048 vMN.1024 vCP.64 vMX.0 vMI.0 vMN.2048 vCP.128 vMX.1024 vMI.1024 vMN.3072 vCP.192",
-        "sA1.3072 sA1.3584 sAB.0 sAB.1024 sXG.0 sAB.2048 sXG.1024 sAB.3072 sXG.2048",
-        "t5HA.0 t7XA.3087 t7MX.3392 t7MX.3776 t7MX.4032", "vMXA.0 vMXA.512 vMXA.1024 vMXA.1536 vMXA.2048 vMXA.2560 vMXA.3072 vMXA.3456 vMXA.3840"]
+ENG = {"FL": "vv", "VAP": "v", "TV": "s", "TA": "s", "TC": "v", "KT": "s", "QQ": "s", "KU": "s", "OWN": "vv", "ARR": "vv"}
+OFF = 24.5
+CG = [(0, 64, "s"), (64, 96, "v"), (96, 128, "s"), (128, 192, "s"), (192, 256, "s")]
+GAM, SCT, CYC, PEC, LAT, LAS, SF, GF = 1.56, 3.8, 0.000833, 0.00044, 0.22, 0.08, 0.09, 0.25
+SND, ARR, ARC, SLOW, SHARE = 1.5, 3.4, 0.003, {"r": 1.0, "n": 1.0}, 0.7
+CASES = [(0.11, 0.2, 0), (0.24, 0.06, 1)]
+ROUNDS, SLACK, SWAPS, HEAT, SEED = 3000, 0.5, 45000, 0.15, 2
+RUNS = []
 ORDER = {}
 M23, M27, M35, M19 = 1.5 * 2.0 ** 23, 1.5 * 2.0 ** 27, 1.5 * 2.0 ** 35, 1.5 * 2.0 ** 19
 
@@ -47,13 +49,14 @@ _sb(WP, "float32", "TT")
 _sb(WP, "bfloat16", "XX")
 _sb(256, "int32", "REQ RR CC FF")
 _sb(W, "float16", "DC HH")
-_sb(256, "bfloat16", "AIM WT HB HA Z ZO FL QQ KT")
+_sb(256, "bfloat16", "AIM WT HB HA Z ZO FL QQ KT KS M2")
 _sb(256, "float16", "WZ CF HF CG HG")
 _sb(256, "float32", "YC SQ KU TC TV TA CT")
 _sb(256, "uint16", "C16")
 _sb(1, "int32", "MUL TH")
 _sb(1, "float32", "THH THS KF ODC OB")
-_sb(2048, "bfloat16", "ONES EB")
+_sb(2048, "bfloat16", "EB")
+_sb(1024, "bfloat16", "ONES")
 _sb(144, "bfloat16", "WS0 WS1 WSB WSM WSG")
 _sb(144, "float16", "WSF")
 _sb(128, "bfloat16", "BM0 BM BMH BMJ BMW IDP IDN IDK IDM IDH IDQ ID2 ID4 ID7 ID8 I7N IBG OD")
@@ -162,6 +165,7 @@ def schedule(ops, preds):
         return st
 
     zero, tail = [0.0] * n, [dur[i] - occ[i] for i in range(n)]
+    suc = [[j for j, _ in l] for l in bw]
     cnt = [len(l) for l in fw]
     run = [i for i in range(n) if cnt[i] == 0]
     for i in run:
@@ -202,6 +206,88 @@ def schedule(ops, preds):
             if e < end:
                 best, end = st, e
     order = sorted(range(n), key=lambda x: (best[x], x))
+
+    seen = [0] * n
+    for i in run:
+        far = 0
+        for j, _ in fw[i]:
+            if preds[i][j]:
+                far |= seen[j]
+        fw[i] = [(j, l) for j, l in fw[i] if not far >> j & 1]
+        seen[i] = far | sum(1 << j for j, _ in fw[i] if preds[i][j])
+    slow = [o * SLOW["r"] if ops[i]["k"] == "r" else o for i, o in enumerate(occ)]
+    more = [dur[i] * (SLOW.get(ops[i]["k"], 1) - 1) for i in range(n)]
+    cases = [([[(j, l + c * more[j] + (0.0 if not preds[i][j] else a - LAT if eng[i] != eng[j] else b - LAS)) for j, l in fw[i]]
+               for i in range(n)], slow if c else occ, a) for a, b, c in CASES]
+
+    def both(order, k, old):
+        r = [play(order, k, old[c][1], old[c][2], *cases[c]) for c in (0, 1)]
+        return (1 - SHARE) * r[0][0] + SHARE * r[1][0], r
+
+    def play(order, k, st, why, fw, occ, LAT):
+        st, why = list(st), list(why)
+        free, banks = {}, [{} for _ in range(8)]
+        for i in order[max(0, k - 150):k]:
+            free[eng[i]] = i
+            for b in bk[i]:
+                banks[b][eng[i]] = i
+        for i in order[k:]:
+            t, w = 0.0, None
+            for j, l in fw[i]:
+                if st[j] + l > t:
+                    t, w = st[j] + l, (j, False)
+            e = eng[i]
+            if e != "n":
+                j = free.get(e)
+                if j is not None and st[j] + occ[j] > t + 1e-9:
+                    t, w = st[j] + occ[j], (j, True)
+                free[e] = i
+                for b in bk[i]:
+                    for e2, j in banks[b].items():
+                        if e2 != e and st[j] + occ[j] + LAT > t + 1e-9:
+                            t, w = st[j] + occ[j] + LAT, (j, True)
+                    banks[b][e] = i
+            st[i], why[i] = t, w
+        i = max(order[-30:], key=lambda x: st[x] + dur[x])
+        end, links = st[i] + dur[i], []
+        while why[i]:
+            if why[i][1]:
+                links.append((why[i][0], i))
+            i = why[i][0]
+        return end, st, why, links
+
+    cur = order
+    blank = [(0, zero, [None] * n)] * 2
+    cend, state = both(cur, 0, blank)
+    end = cend
+    for it in range(SWAPS):
+        links = state[rnd() < 0.5][3]
+        a, b = links[int(rnd() * len(links))]
+        pa, pb = cur.index(a), cur.index(b)
+        if rnd() < 0.5:
+            pa = max(0, pa - (int(12 * rnd()) if rnd() < 0.3 else 0))
+            mv = {b}
+            for x in cur[pb - 1:pa - 1 if pa else None:-1]:
+                if not mv.isdisjoint(suc[x]):
+                    mv.add(x)
+            front = True
+        else:
+            pb = min(n - 1, pb + (int(12 * rnd()) if rnd() < 0.3 else 0))
+            mv = {a}
+            for x in cur[pa + 1:pb + 1]:
+                if not mv.isdisjoint(preds[x]):
+                    mv.add(x)
+            front = False
+        if a in mv and b in mv:
+            continue
+        seg = cur[pa:pb + 1]
+        new = cur[:pa] + [x for x in seg if (x in mv) == front] + [x for x in seg if (x in mv) != front] + cur[pb + 1:]
+        r = both(new, pa, state)
+        if r[0] <= cend - HEAT * (1.0 - it / SWAPS) * math.log(rnd() + 1e-9):
+            cur, (cend, state) = new, r
+            if cend < end:
+                order, end = cur, cend
+    end, best = both(order, 0, blank)[1][0][:2]
     extra, user = [[] for _ in range(n)], {}
     for i in order:
         for b in bk[i]:
@@ -289,6 +375,15 @@ def build(g, T, core, topo):
         else:
             act(out, i, F.Identity, bias=bias, scale=scale)
 
+    table, silu = [1.3], "s" in ENG["OWN"] + ENG["ARR"]
+
+    def put(e, out, i):
+        if e == "v":
+            vcp(out, i)
+        else:
+            add("s", [lambda: g.scalar.activation(ap(out), ap(i), F.Silu)], size(i) * SCT * CYC + 0.065 + table[0], [i], [out])
+            table[0] = 0.0
+
     tails = {}
 
     def chain(name):
@@ -321,7 +416,7 @@ def build(g, T, core, topo):
         add(e, [lambda: q[e].dma_start(out, i)], cost, R, W_, "d", 0.1, s, 16)
 
     def gsel(out, i, pat, op, base, cm):
-        add("g", [lambda: g.affine_select(ap(out), ap(i), pat, op, 0.0, base, cm)], 0.17 + 2 * size(out) * CYC, [i], [out])
+        add("g", [lambda: g.affine_select(ap(out), ap(i), pat, op, 0.0, base, cm)], GF + 2 * size(out) * CYC, [i], [out])
 
     def gio(out, pat, base, cm):
         add("g", [lambda: g.iota(ap(out), pat, base, cm)], 0.16, (), [out])
@@ -350,12 +445,13 @@ def build(g, T, core, topo):
     gio(X("PRI"), [[0, 16]], 0, 1)
     gio(X("I256"), [[256, 16]], 0, 0)
     gio(X("I16"), [[16, 16]], W, 0)
-    gsel(X("EB", 0, 16 * (KH - KL)), X("ONES", 0, 16 * (KH - KL)), [[-1, KH - KL], [0, 16]], A.is_equal, 0, 1)
+    for k in (0, 64):
+        gsel(X("EB", 16 * k, 16 * k + 1024), X("ONES", 0, 1024), [[-1, 64], [0, 16]], A.is_equal, -k, 1)
     gsel(X("BM0"), X("ONES", 0, 128), [[-16, 8], [0, 16]], A.is_ge, 0, 1)
     gsel(X("BM"), X("BM0"), [[16, 8], [0, 16]], A.is_ge, 15, -1)
     gsel(X("WS1"), X("WS0"), [[-1, 144]], A.is_ge, 15, 1)
     gsel(X("WSB"), X("WS1"), [[1, 144]], A.is_ge, 0, -1)
-    for nm, c in (("ID4", 4096.0), ("ID7", 7.5), ("IDN", -1.0), ("IDK", 2.0 ** -14), ("I32", 1.0), ("IDM", -(2.0 ** -14)),
+    for nm, c in (("ID4", 4096.0), ("ID7", -OFF), ("IDN", -1.0), ("IDK", 2.0 ** -14), ("I32", 1.0), ("IDM", -(2.0 ** -14)),
                   ("IDH", 0.5), ("IDQ", -0.25), ("I7N", -7.5), ("IBG", M19), ("ID2", 2048.0), ("ID8", 8192.0)):
         act(X(nm), X("IDP"), F.Copy, scale=c)
     vcp(X("IDF"), X("IDP"))
@@ -369,6 +465,13 @@ def build(g, T, core, topo):
     if JS < 16:
         gsel(X("BMJ"), X("BMH"), [[0, 8], [-1, 16]], A.is_ge, JS - 1, 0)
 
+    def turn(name, lo, hi):
+        n = hi - lo
+        P, P2 = X("b5", 256, 384, 1, n), X("b5", 384, 512, 1, n)
+        mm([(P, X("CF", lo, hi), X("IDF")), (P, X("HB", lo, hi), X("IDN")), (P2, X("HB", lo, hi), X("IDP"))])
+        aff("KT", X(name, 0, 128, 1, n), P, -1.0, -2048.0)
+        aff("KT", X(name, 128, 256, 1, n), P2, -(2.0 ** -14), 0.0)
+
     def forms(src, lo, hi):
         vts(X("CF", lo, hi), X(src, lo, hi), -2048.0, None, A.add)
         vts(X("C16", lo, hi), X("CF", lo, hi), 2048.0, None, A.add)
@@ -376,26 +479,32 @@ def build(g, T, core, topo):
         vts(X("HB", lo, hi), X("HF", lo, hi), -24576.0, None, A.add)
         for h in SPR:
             l, e = SPR[h]
+            e = "gggg" if src == "REQ" else e
             if not lo < h <= hi:
+                continue
+            if e == "p":
+                n = h - l
+                turn("KS", l, h)
+                for a in range(0, 16 * n, 1024):
+                    for b in (0, 512):
+                        x = X("EB", a + b, a + b + 512, 1, n)
+                        mm([(X("b1", b, b + 512), X("KS", c, c + 128, 1, n), x) for c in (0, 128)])
+                    act(X("CKB", 16 * l + a, 16 * l + a + 1024), X("b1", 0, 1024), F.Identity, bias=OFF, scale=-1.0)
                 continue
             P = X("b5", l, h)
             mm([(P, X("IDF"), X("CF", l, h)), (P, X("IDN"), X("HB", l, h)), (P, X("IDK"), X("HB", l, h))])
-            aff("TC", X("TC", l, h), P, 1.0, 2040.5)
+            aff("TC", X("TC", l, h), P, 1.0, 2048 + OFF)
             o, i = [ap(X("CKB", 16 * l + j, 16 * h, 16)) for j in range(16)], ap(X("TC", l, h))
             for j in range(0, 16, 4):
                 wr = [X("CKB", 16 * l + k, 16 * h, 16) for k in range(j, j + 4)]
                 if e[j // 4] == "g":
                     add("g", [(lambda x=x, i=i, n=h - l: g.affine_select(x, i, [[0, n]], A.is_equal, 0.0, 0, 0)) for x in o[j:j + 4]],
-                        4 * (0.17 + 2 * (h - l) * CYC), [X("TC", l, h)], wr)
+                        4 * (GF + 2 * (h - l) * CYC), [X("TC", l, h)], wr)
                 else:
                     add("s", [(lambda x=x, i=i: g.scalar.activation(x, i, F.Copy)) for x in o[j:j + 4]],
                         4 * (SF + (h - l) * CYC), [X("TC", l, h)], wr)
         if lo < KH <= hi:
-            n = KH - KL
-            P, P2 = X("b5", 256, 384, 1, n), X("b5", 384, 512, 1, n)
-            mm([(P, X("CF", KL, KH), X("IDF")), (P, X("HB", KL, KH), X("IDN")), (P2, X("HB", KL, KH), X("IDP"))])
-            aff("KT", X("KT", 0, 128, 1, n), P, -1.0, -2048.0)
-            aff("KT", X("KT", 128, 256, 1, n), P2, -(2.0 ** -14), 0.0)
+            turn("KT", KL, KH)
 
     for lo, hi in CN:
         forms("REQ", lo, hi)
@@ -412,15 +521,15 @@ def build(g, T, core, topo):
             vts(X("HH", l0, h0), X("DC", l0, h0), 2048 + 24576 - 7.5, None, A.add)
             vts(X("HT", l0, h0), X("HH", l0, h0), -24576.0, None, A.add)
             mm([(P2, X("IDF"), X("DC", l0, h0))] + ht)
-            act(X("TT", l0, h0), P2, F.Identity, bias=2040.5)
+            act(X("TT", l0, h0), P2, F.Identity, bias=2048 + OFF)
             continue
         mm([(P, X("ID7"), X("ONES", 0, 512)), (P, X("ID4"), X("XX", l0, h0))])
         vtt(X("A2", l0, h0), X("REC", l0, h0), P, A.subtract)
         if UM[k] == "s":
             act(X("A1", l0, h0), X("A2", l0, h0), F.Identity, bias=M27)
-            act(X("HT", l0, h0), X("A1", l0, h0), F.Identity, bias=-M27)
+            act(X("HT", l0, h0), X("A1", l0, h0), F.Identity, bias=-M27 - 32)
         else:
-            vts(X("HT", l0, h0), X("A2", l0, h0), M27, -M27, A.add, A.add)
+            vts(X("HT", l0, h0), X("A2", l0, h0), M27, -M27 - 32, A.add, A.add)
         mm(ht)
         vtt(X("TT", l0, h0), X("A2", l0, h0), P2, A.add)
     vts(X("THH"), X("TH"), 0.5, None, A.mult)
@@ -456,7 +565,7 @@ def build(g, T, core, topo):
             add("g", [lambda: g.remote_dma(ap(out), ap(src), T.sem[rs], T.sem[ls], pid, rid, msk)], SND, [src], [tok], "r", SND, ls, ne,
                 chain("send"))
             ops[-1]["tag"] = "gsend." + m
-            add("n", [], ARR, [tok], [out], "n", 0.0, rs, ne)
+            add("n", [], ARR + ARC * size(src), [tok], [out], "n", 0.0, rs, ne)
 
         for lo, hi in C1:
             el, eh = 16 * lo, 16 * hi
@@ -472,17 +581,20 @@ def build(g, T, core, topo):
                 P = X("b1", o + l - l0, o + l - l0 + PU)
                 e = X("EB", l - 16 * KL, l + PU - 16 * KL, 1, KH - KL)
                 mm([(P, X("KT", 0, 128, 1, KH - KL), e), (P, X("KT", 128, 256, 1, KH - KL), e), (P, X("I32"), X("A1", l, l + PU))])
-            act(X("AB", l0, l0 + AU), X("b1", o, o + AU), F.Abs, bias=4080.0 - 7.5 * 16384, scale=-16384.0)
+            act(X("AB", l0, l0 + AU), X("b1", o, o + AU), F.Abs, bias=4080.0 + OFF * 16384, scale=-16384.0)
         for lo, hi in C1S:
             n = 16 * (hi - lo)
             el, eh = 16 * lo, 16 * hi
             vscan(X("MN", el, eh), X("MSN", 0, n), X("AB", el, eh), A.max, A.min)
             mn = X("MN", el + 15, eh, 16)
+            if silu:
+                vts(X("M2", lo, hi), mn, M27, -M27, A.add, A.add)
+                mn = X("M2", lo, hi)
             if hi in CPV:
                 vtt(X("CT", lo, hi), X("CF", lo, hi), mn, A.subtract)
                 vts(X(CP, lo, hi), X("CT", lo, hi), 2048.0 + 4080.0, None, A.add)
             else:
-                P = X("b3", lo, hi)
+                P = X(("b3", "b6")[lo // 64 % 2], lo, hi)
                 mm([(P, X("IDF"), X("CF", lo, hi)), (P, X("IDN"), mn)])
                 vts(X(CP, lo, hi), P, 2048.0 + 4080.0, None, A.add)
             if hi in SC:
@@ -490,8 +602,8 @@ def build(g, T, core, topo):
         if not last:
             P = X("b4", 0, 256)
             mm([(P, X("IDF"), X("CF")), (P, X("IDN"), X("HB")), (P, X("IDK"), X("HB"))], True, False)
-            mm([(P, X("IDM"), X("MN", 15, W, 16))], False, True)
-            aff("TV", X("TV"), P, 1.0, 2040.5 + 4080.0 / 16384)
+            mm([(P, X("IDM"), X("M2") if silu else X("MN", 15, W, 16))], False, True)
+            aff("TV", X("TV"), P, 1.0, 2048 + OFF + 4080.0 / 16384)
         for lo, hi, e in C2:
             n = 16 * (hi - lo)
             el, eh = 16 * lo, 16 * hi
@@ -506,7 +618,7 @@ def build(g, T, core, topo):
                 vtt(X("WZ", lo, hi), X("FF", lo, hi), X("b0", lo, hi), A.mult)
                 vcp(X("Z", lo, hi), X("FF", lo, hi))
                 continue
-            P = X("b3", 256 + lo, 256 + hi)
+            P = X(("b6", "b3")[lo // 64 % 2], 256 + lo, 256 + hi)
             mm([(P, X("IDQ"), X("ONES", 0, hi - lo)), (P, X("IDH"), X("MX", el + 15, eh, 16)), (P, X("IDH"), X("MI", el + 15, eh, 16))])
             vts(X("Z", lo, hi), P, M23, -M23 - 128, A.add, A.add)
             vtt(X("WZ", lo, hi), X("Z", lo, hi), X("b0", lo, hi), A.mult)
@@ -534,7 +646,7 @@ def build(g, T, core, topo):
         for lo, hi in GR:
             vcp(ind(X("XX", 0, W), X("P16", lo // 16, hi // 16)), X(VN, lo, hi))
             if not last:
-                vcp(ind(X("TT", 0, W), X("P16", lo // 16, hi // 16)), X("TV", lo, hi))
+                put(ENG["OWN"][lo > 0], ind(X("TT", 0, W), X("P16", lo // 16, hi // 16)), X("TV", lo, hi))
         if last:
             vts(X("ZO"), X("Z"), 128.0, None, A.add)
             dma("y", T.yz[:], T.ZO[:], 2.5, [X("ZO")], [("yz", 0, 1, 1, 128)])
@@ -562,9 +674,9 @@ def build(g, T, core, topo):
             vts(X("CG"), X(CA), -2048.0, None, A.add)
             vts(X("HG"), X("CG"), 2048 + 24576 - 7.5, None, A.add)
             vts(X("HA"), X("HG"), -24576.0, None, A.add)
-            P = X("b5", 0, 256)
+            P = X("b3", 256, 512)
             mm([(P, X("IDF"), X("CG")), (P, X("IDN"), X("HA")), (P, X("IDK"), X("HA"))])
-            aff("TA", X("TA"), P, 1.0, 2040.5)
+            aff("TA", X("TA"), P, 1.0, 2048 + OFF)
         for lo, hi in SV:
             hi = max([lo] + [c[1] for c in C3 if c[1] - c[0] > 32 and c[3] and c[1] <= hi])
             if hi == lo:
@@ -579,7 +691,9 @@ def build(g, T, core, topo):
             m = hi - lo
             el, eh = 16 * lo, 16 * hi
             va = X(VA, lo, hi)
-            gather(e, X("XA", el, eh), ind(X("XX", 0, W), X(CA, lo, hi)), chain("x" + e))
+            for l, h, e in CG:
+                if lo <= l < hi:
+                    gather(e, X("XA", 16 * l, 16 * h), ind(X("XX", 0, W), X(CA, l, h)), chain("x" + e))
             D = X("b%d" % (6, 4, 2, 7, 6)[c], 0, m)
             xa = [X("XA", el + j, eh, 16) for j in range(16)]
             mx = [X("MXA", el + m * j, el + m * j + m) for j in range(16)]
@@ -607,7 +721,7 @@ def build(g, T, core, topo):
                 continue
             lo = 0 if hi == SB else SB
             wl, wh = lo // 16, hi // 16
-            P = X("b3", 480 + wl, 480 + wh)
+            P = X("b6", 480 + wl, 480 + wh)
             mm([(P, X("ID8"), X("ONES", 0, wh - wl))] * (fe == "s") + [(P, sel("WSG", r), X("FL", lo + r, hi, 16)) for r in range(16)])
             dum = "DUL" if last else "DUM"
             if lo == 0:
@@ -616,9 +730,9 @@ def build(g, T, core, topo):
                 vcp(X("O16", wl, wh), X("OG", wl, wh))
             else:
                 for w in range(wl, wh):
-                    vts(X("O16", w, w + 1), X("b3", 480 + w, 481 + w), X("PD", w, w + 1), X(dum, w, w + 1), A.max, A.min)
+                    vts(X("O16", w, w + 1), X("b6", 480 + w, 481 + w), X("PD", w, w + 1), X(dum, w, w + 1), A.max, A.min)
             if not last:
-                vcp(ind(X("TT"), X("O16", wl, wh)), X("TA", lo, hi))
+                put(ENG["ARR"][lo > 0], ind(X("TT"), X("O16", wl, wh)), X("TA", lo, hi))
         for lo, hi in ((0, SB), (SB, 256)):
             vcp(ind(X("XX", 16 * lo if last else 0, WP), X("O16", lo // 16, hi // 16)), X(VA, lo, hi))
             if last:

import math
from concourse.mybir import dt, AluOpType, AxisListType, ActivationFunctionType

A = AluOpType
F = ActivationFunctionType
STEPS = 3
W = 4096
WP = W + 256
KL, KH = 192, 256
SP = 192
C1 = [(0, 64), (64, 128), (128, 192), (192, 224), (224, 256)]
C1S = [(0, 64), (64, 128), (128, 192), (192, 256)]
C2 = [(0, 32, "v"), (32, 64, "s"), (64, 128, "s"), (128, 192, "s"), (192, 224, "s"), (224, 256, "s")]
C3 = [(0, 64, "s", 16), (64, 128, "s", 16), (128, 192, "s", 16), (192, 256, "s", 16)]
SC = {128: 0, 256: 128}
SV = [(0, 128), (128, 192), (192, 256)]
CN = [(0, 192), (192, 256)]
SPR = {192: (0, "ggss")}
SB = 192
PU, AU = 256, 512
UNP = [512] * 8
UM = "sdsddsdv"
CPV = ()
CZ = [(0, 64, "t"), (64, 128, "t"), (128, 192, "t"), (192, 256, "t")]
CV = [(0, 128), (128, 192), (192, 256)]
ENG = {"FL": "vv", "VAP": "v", "TV": "s", "TA": "s", "TC": "v", "KT": "s", "QQ": "s", "KU": "s", "OWN": "vv", "ARR": "vv"}
OFF = 24.5
CG = [(0, 64, "s"), (64, 96, "v"), (96, 128, "s"), (128, 192, "s"), (192, 256, "s")]
GAM, SCT, CYC, PEC, LAT, LAS, SF, GF = 1.56, 3.8, 0.000833, 0.00044, 0.22, 0.08, 0.09, 0.25
SND, ARR, ARC, SLOW, SHARE = 1.5, 3.4, 0.003, {"r": 1.0, "n": 1.0}, 0.7
CASES = [(0.11, 0.2, 0), (0.24, 0.06, 1)]
ROUNDS, SLACK, SWAPS, HEAT, SEED = 3000, 0.5, 45000, 0.15, 2
RUNS = []
ORDER = {}
M23, M27, M35, M19 = 1.5 * 2.0 ** 23, 1.5 * 2.0 ** 27, 1.5 * 2.0 ** 35, 1.5 * 2.0 ** 19

SCRATCH = {"b": ("psum", [128, 4096], "float32")}


def _sb(cols, dtype, names):
    for n in names.split():
        SCRATCH[n] = ("sbuf", [128, cols], dtype)


_sb(W, "int32", "REC")
_sb(W, "float32", "A2 A1 CKB")
_sb(W, "bfloat16", "HT U1 AB MN XG MX MI XA MXA")
_sb(WP, "float32", "TT")
_sb(WP, "bfloat16", "XX")
_sb(256, "int32", "REQ RR CC FF")
_sb(W, "float16", "DC HH")
_sb(256, "bfloat16", "AIM WT HB HA Z ZO FL QQ KT KS M2")
_sb(256, "float16", "WZ CF HF CG HG")
_sb(256, "float32", "YC SQ KU TC TV TA CT")
_sb(256, "uint16", "C16")
_sb(1, "int32", "MUL TH")
_sb(1, "float32", "THH THS KF ODC OB")
_sb(2048, "bfloat16", "EB")
_sb(1024, "bfloat16", "ONES")
_sb(144, "bfloat16", "WS0 WS1 WSB WSM WSG")
_sb(144, "float16", "WSF")
_sb(128, "bfloat16", "BM0 BM BMH BMJ BMW IDP IDN IDK IDM IDH IDQ ID2 ID4 ID7 ID8 I7N IBG OD")
_sb(128, "float16", "IDF BF")
_sb(128, "float32", "I32")
_sb(1024, "bfloat16", "MSN MSX")
_sb(16, "int32", "PRI PR I256 I16 R16")
_sb(16, "float32", "BASE BASL DUM DUL FU PI PD OF OG")
_sb(16, "uint16", "P16 O16")
for _t in range(STEPS):
    _sb(256, "uint16", "CP%d CA%d" % (_t, _t))
    _sb(272, "bfloat16", "VN%d VA%d" % (_t, _t))
SEMAPHORES = ["sv", "ss", "st", "sg"] + ["d%d" % k for k in range(24)] + \
    ["%s%d%s" % (m, t, x) for m in ("c", "e", "u", "v", "w") for t in range(STEPS) for x in ("l", "r")]


def X(name, lo=0, hi=None, step=1, parts=128):
    if name[0] == "b":
        o = 512 * int(name[1])
        return ("b", o + lo, o + (512 if hi is None else hi), step, parts)
    return (name, lo, SCRATCH[name][1][1] if hi is None else hi, step, parts)


def ind(win, off):
    return ("@", win, off)


def size(a):
    return (a[2] - a[1] + a[3] - 1) // a[3]


def plan(ops):
    hist = {}
    preds = []
    for i in range(len(ops)):
        o = ops[i]
        d = {}
        for j in o["after"]:
            d[j] = False
        for acc, wr in [(a, False) for a in o["R"]] + [(a, True) for a in o["W"]]:
            for lo, hi, j, w, sp in hist.get(acc[0], ()):
                if sp > 1 and sp == acc[3] and (lo - acc[1]) % sp:
                    continue
                if j != i and lo < acc[2] and acc[1] < hi and (w or wr):
                    sync = w or ops[j]["e"] != o["e"] or ops[j]["k"] != "c"
                    if w and wr and ops[j]["e"] == "t" and o["e"] == "t":
                        sync = False
                    d[j] = d.get(j, False) or sync
        for a in o["W"]:
            h = hist.get(a[0], [])
            if a[3] == 1 and a[4] == 128:
                h = [x for x in h if not (a[1] <= x[0] and x[1] <= a[2])]
            elif a[4] == 128:
                h = [x for x in h if x[:2] != a[1:3] or x[4] != a[3]]
            hist[a[0]] = h + [(a[1], a[2], i, True, a[3])]
        for a in o["R"]:
            hist.setdefault(a[0], []).append((a[1], a[2], i, False, a[3]))
        preds.append(d)
    return preds


def schedule(ops, preds):
    n = len(ops)
    occ, dur, eng, bk = [[o[x] for o in ops] for x in ("occ", "dur", "e", "B")]
    fw = [[(j, dur[j] + (LAT if eng[i] != eng[j] else LAS) if preds[i][j] else occ[j]) for j in preds[i]] for i in range(n)]
    bw = [[] for _ in range(n)]
    for i in range(n):
        for j, l in fw[i]:
            bw[j].append((i, occ[i] + l - occ[j]))

    def place(key, lags, run, rel):
        for i in run:
            for j, _ in lags[i]:
                if key[i] <= key[j]:
                    key[i] = key[j] + 1e-7
        st = [0.0] * n
        busy = {e: ([], []) for e in eng}
        banks = [[] for b in range(8)]
        for _, i in sorted(zip(key, range(n))):
            t = rel[i]
            for j, l in lags[i]:
                if st[j] + l > t:
                    t = st[j] + l
            e, o = eng[i], occ[i]
            if e != "n":
                S, E = busy[e]
                while True:
                    t0 = t
                    k = len(E)
                    while k and E[k - 1] > t + 1e-9:
                        k -= 1
                    while k < len(S) and S[k] < t + o - 1e-9:
                        t = E[k]
                        k += 1
                    for b in bk[i]:
                        for f, s, e2 in banks[b][-12:]:
                            if f > t and s < t + o and e2 != e:
                                t = f
                    if t == t0:
                        break
                S.insert(k, t)
                E.insert(k, t + o)
                for b in bk[i]:
                    banks[b].append((t + o + LAT, t - LAT, e))
            st[i] = t
        return st

    zero, tail = [0.0] * n, [dur[i] - occ[i] for i in range(n)]
    suc = [[j for j, _ in l] for l in bw]
    cnt = [len(l) for l in fw]
    run = [i for i in range(n) if cnt[i] == 0]
    for i in run:
        for j, _ in bw[i]:
            cnt[j] -= 1
            if cnt[j] == 0:
                run.append(j)
    assert len(run) == n

    def forward(key):
        st = place(key, fw, run, zero)
        return st, max(st[i] + dur[i] for i in range(n))

    def again(st):
        r = place([-(st[i] + occ[i]) for i in range(n)], bw, run[::-1], tail)
        return forward([-(r[i] + occ[i]) for i in range(n)])

    bl = [0.0] * n
    for i in run[::-1]:
        bl[i] = dur[i] + max([bl[j] + LAT for j, _ in bw[i]] + [0.0])
    best, end = again(forward([-b for b in bl])[0])
    cur, cend = best, end
    seed = [SEED]

    def rnd():
        seed[0] = (seed[0] * 1103515245 + 12345) % 2147483648
        return seed[0] / 2147483648.0
    for it in range(ROUNDS):
        c, w, a = rnd() * end, 1.0 + 7.0 * rnd(), 4.0 * rnd() ** 2
        only = "vstg"[int(4 * rnd())] if rnd() < 0.5 else None
        shake = {ops[i]["tag"]: a * (rnd() - 0.5) for i in range(n) if abs(cur[i] - c) < w and only in (None, eng[i])}
        every = rnd() < 0.7
        st, e = forward([cur[i] + (shake.get(ops[i]["tag"], 0.0) if every or abs(cur[i] - c) < w else 0.0) for i in range(n)])
        if e < cend + 1.0:
            st, e = again(st)
        if e <= cend + SLACK * (1.0 - it / ROUNDS) * rnd():
            cur, cend = st, e
            if e < end:
                best, end = st, e
    order = sorted(range(n), key=lambda x: (best[x], x))

    seen = [0] * n
    for i in run:
        far = 0
        for j, _ in fw[i]:
            if preds[i][j]:
                far |= seen[j]
        fw[i] = [(j, l) for j, l in fw[i] if not far >> j & 1]
        seen[i] = far | sum(1 << j for j, _ in fw[i] if preds[i][j])
    slow = [o * SLOW["r"] if ops[i]["k"] == "r" else o for i, o in enumerate(occ)]
    more = [dur[i] * (SLOW.get(ops[i]["k"], 1) - 1) for i in range(n)]
    cases = [([[(j, l + c * more[j] + (0.0 if not preds[i][j] else a - LAT if eng[i] != eng[j] else b - LAS)) for j, l in fw[i]]
               for i in range(n)], slow if c else occ, a) for a, b, c in CASES]

    def both(order, k, old):
        r = [play(order, k, old[c][1], old[c][2], *cases[c]) for c in (0, 1)]
        return (1 - SHARE) * r[0][0] + SHARE * r[1][0], r

    def play(order, k, st, why, fw, occ, LAT):
        st, why = list(st), list(why)
        free, banks = {}, [{} for _ in range(8)]
        for i in order[max(0, k - 150):k]:
            free[eng[i]] = i
            for b in bk[i]:
                banks[b][eng[i]] = i
        for i in order[k:]:
            t, w = 0.0, None
            for j, l in fw[i]:
                if st[j] + l > t:
                    t, w = st[j] + l, (j, False)
            e = eng[i]
            if e != "n":
                j = free.get(e)
                if j is not None and st[j] + occ[j] > t + 1e-9:
                    t, w = st[j] + occ[j], (j, True)
                free[e] = i
                for b in bk[i]:
                    for e2, j in banks[b].items():
                        if e2 != e and st[j] + occ[j] + LAT > t + 1e-9:
                            t, w = st[j] + occ[j] + LAT, (j, True)
                    banks[b][e] = i
            st[i], why[i] = t, w
        i = max(order[-30:], key=lambda x: st[x] + dur[x])
        end, links = st[i] + dur[i], []
        while why[i]:
            if why[i][1]:
                links.append((why[i][0], i))
            i = why[i][0]
        return end, st, why, links

    cur = order
    blank = [(0, zero, [None] * n)] * 2
    cend, state = both(cur, 0, blank)
    end = cend
    for it in range(SWAPS):
        links = state[rnd() < 0.5][3]
        a, b = links[int(rnd() * len(links))]
        pa, pb = cur.index(a), cur.index(b)
        if rnd() < 0.5:
            pa = max(0, pa - (int(12 * rnd()) if rnd() < 0.3 else 0))
            mv = {b}
            for x in cur[pb - 1:pa - 1 if pa else None:-1]:
                if not mv.isdisjoint(suc[x]):
                    mv.add(x)
            front = True
        else:
            pb = min(n - 1, pb + (int(12 * rnd()) if rnd() < 0.3 else 0))
            mv = {a}
            for x in cur[pa + 1:pb + 1]:
                if not mv.isdisjoint(preds[x]):
                    mv.add(x)
            front = False
        if a in mv and b in mv:
            continue
        seg = cur[pa:pb + 1]
        new = cur[:pa] + [x for x in seg if (x in mv) == front] + [x for x in seg if (x in mv) != front] + cur[pb + 1:]
        r = both(new, pa, state)
        if r[0] <= cend - HEAT * (1.0 - it / SWAPS) * math.log(rnd() + 1e-9):
            cur, (cend, state) = new, r
            if cend < end:
                order, end = cur, cend
    end, best = both(order, 0, blank)[1][0][:2]
    extra, user = [[] for _ in range(n)], {}
    for i in order:
        for b in bk[i]:
            extra[i] += [j for e2, j in user.get(b, {}).items() if e2 != eng[i]]
            user.setdefault(b, {})[eng[i]] = i
    return order, best, end, extra


def build(g, T, core, topo):
    ops = []
    q = {"v": g.vector, "s": g.scalar, "t": g.tensor, "g": g, "y": g.sync}

    def ap(a):
        if not isinstance(a, tuple):
            return a
        if a[0] == "@":
            return ap(a[1]).indirect(ap(a[2]))
        return T[a[0]][0:a[4], a[1]:a[2]:a[3]] if a[3] > 1 else T[a[0]][0:a[4], a[1]:a[2]]

    def parts(l):
        r = []
        for a in l:
            if isinstance(a, tuple):
                r += [a[1], a[2]] if a[0] == "@" else [a]
        return r

    def add(e, calls, cost, R, W_, k="c", occ=None, sem=None, val=0, after=()):
        R = parts(R)
        nm = W_[0]
        for a in W_:
            if a[0] == "@":
                R.append(a[2])
                nm = (a[1][0] + a[2][0], a[2][1])
        W_ = [a[1] if a[0] == "@" else a for a in W_]
        B = sorted(set(k for a in R + W_ if a[0] == "b" for k in range(a[1] // 512, (a[2] + 511) // 512)))
        if e == "t":
            nm = ("%d" % B[0] + R[-1][0][:2], R[-1][1])
        name = nm[0][:2] if nm[0][:2] in ("CP", "CA", "TV", "TA", "VN", "VA") else nm[0]
        ops.append({"tag": "%s%s.%s" % (e, name, nm[1]), "e": e, "f": calls, "dur": cost,
                    "occ": cost if occ is None else occ, "R": R, "W": W_, "B": B, "k": k, "sem": sem, "val": val, "after": list(after)})

    def narrow(*l):
        return all(SCRATCH[a[0]][2] in ("bfloat16", "float16", "uint16") for a in l)

    def vcost(out, i):
        if i[0] == "@":
            return size(out) * GAM * CYC + 0.05
        if out[0] == "@":
            return size(i) * SCT * CYC + 0.05
        return max(64, size(out) * (0.5 if narrow(out, i) else 1.0)) * CYC

    def vts(out, i, s1, s2, op0, op1=None):
        if op1 is None:
            f = lambda: g.vector.tensor_scalar(ap(out), ap(i), ap(s1), None, op0)
        else:
            f = lambda: g.vector.tensor_scalar(ap(out), ap(i), ap(s1), ap(s2), op0, op1)
        add("v", [f], vcost(out, i), [i, s1, s2], [out])

    def vtts(lst, op):
        c = 0.0
        for out, a, b in lst:
            c += vcost(out, a) if a[0] == "@" else max(64, size(out) * (1.0 if "b" in (a[0][0], b[0][0]) else 2.0)) * CYC
        add("v", [(lambda o=o, a=a, b=b: g.vector.tensor_tensor(ap(o), ap(a), ap(b), op)) for o, a, b in lst], c,
            [x for o, a, b in lst for x in (a, b)], [o for o, a, b in lst])

    def vtt(out, a, b, op):
        vtts([(out, a, b)], op)

    def vcp(out, i):
        add("v", [lambda: g.vector.tensor_copy(ap(out), ap(i))], vcost(out, i), [i], [out])

    def vset(out, c):
        add("v", [lambda: g.vector.memset(ap(out), c)], vcost(out, out), (), [out])

    def vscan(out, m, i, op0, op1):
        add("v", [lambda: g.vector.tensor_tensor_scan(ap(out), ap(m), ap(i), 0.0, op0, op1)], vcost(out, i), [m, i], [out])

    def act(out, i, fn, bias=0.0, scale=1.0):
        c = size(out) * GAM * CYC + 0.065 if i[0] == "@" else size(out) * CYC + SF
        add("s", [lambda: g.scalar.activation(ap(out), ap(i), fn, bias=ap(bias), scale=ap(scale))], c, [i, bias, scale], [out])

    def aff(name, out, i, scale, bias):
        if ENG[name] == "v":
            vts(out, i, scale, bias, A.mult, A.add)
        else:
            act(out, i, F.Identity, bias=bias, scale=scale)

    table, silu = [1.3], "s" in ENG["OWN"] + ENG["ARR"]

    def put(e, out, i):
        if e == "v":
            vcp(out, i)
        else:
            add("s", [lambda: g.scalar.activation(ap(out), ap(i), F.Silu)], size(i) * SCT * CYC + 0.065 + table[0], [i], [out])
            table[0] = 0.0

    tails = {}

    def chain(name):
        r = [tails[name]] if name in tails else []
        tails[name] = len(ops)
        return r

    def gather(e, out, i, after=()):
        if e == "v":
            vcp(out, i)
        else:
            act(out, i, F.Copy)
        ops[-1]["after"] = list(after)

    def mm(lst, start=True, stop=True):
        fs, c = [], 0.03
        for k in range(len(lst)):
            o, l, r = lst[k]
            s = start and (k == 0 or lst[k - 1][0] != o)
            p = stop and (k == len(lst) - 1 or lst[k + 1][0] != o)
            fs.append(lambda o=o, l=l, r=r, s=s, p=p: g.tensor.matmul(ap(o), ap(l), ap(r), s, p))
            c += max(64, size(r)) * PEC * (4 if SCRATCH[r[0]][2] == "float32" else 1)
        add("t", fs, c, [x for o, l, r in lst for x in (l, r)], [x[0] for x in lst])

    nd = [0]

    def dma(e, out, i, cost, R, W_):
        s = "d%d" % nd[0]
        nd[0] += 1
        add(e, [lambda: q[e].dma_start(out, i)], cost, R, W_, "d", 0.1, s, 16)

    def gsel(out, i, pat, op, base, cm):
        add("g", [lambda: g.affine_select(ap(out), ap(i), pat, op, 0.0, base, cm)], GF + 2 * size(out) * CYC, [i], [out])

    def gio(out, pat, base, cm):
        add("g", [lambda: g.iota(ap(out), pat, base, cm)], 0.16, (), [out])

    def sel(m, r):
        return X(m, 15 - r, 143 - r)

    UB = [sum(UNP[:k]) for k in range(len(UNP) + 1)]
    dma("y", T.REQ[:], T.req[:], 2.2, (), [X("REQ")])
    for k in range(len(UNP)):
        sl = slice(UB[k], UB[k + 1])
        dma("s" if k % 2 == 0 else "y", T.REC[:, sl], T.rec[:, sl], 2.0 + UB[k + 1] * 0.0016, (), [X("REC", UB[k], UB[k + 1])])
    dma("y", T.MUL[:], T.mul[:], 9.0, (), [X("MUL")])
    dma("y", T.TH[:], T.th[:], 9.0, (), [X("TH")])
    dma("s", T.WT[:], T.wt[:], 9.0, (), [X("WT")])
    dma("s", T.AIM[:], T.aim[:], 9.0, (), [X("AIM")])

    vset(X("ONES"), 1.0)
    vset(X("MSN"), 0.0)
    vset(X("MSX"), 1.0)
    vset(X("MSN", 0, 1024, 16), 4080.0)
    vset(X("MSX", 0, 1024, 16), 0.0)
    vset(X("WS0"), 0.0)
    vset(X("WS0", 15, 144, 16), 1.0)
    gsel(X("IDP"), X("ONES", 0, 128), [[-1, 128]], A.is_equal, 0, 1)
    gio(X("PRI"), [[0, 16]], 0, 1)
    gio(X("I256"), [[256, 16]], 0, 0)
    gio(X("I16"), [[16, 16]], W, 0)
    for k in (0, 64):
        gsel(X("EB", 16 * k, 16 * k + 1024), X("ONES", 0, 1024), [[-1, 64], [0, 16]], A.is_equal, -k, 1)
    gsel(X("BM0"), X("ONES", 0, 128), [[-16, 8], [0, 16]], A.is_ge, 0, 1)
    gsel(X("BM"), X("BM0"), [[16, 8], [0, 16]], A.is_ge, 15, -1)
    gsel(X("WS1"), X("WS0"), [[-1, 144]], A.is_ge, 15, 1)
    gsel(X("WSB"), X("WS1"), [[1, 144]], A.is_ge, 0, -1)
    for nm, c in (("ID4", 4096.0), ("ID7", -OFF), ("IDN", -1.0), ("IDK", 2.0 ** -14), ("I32", 1.0), ("IDM", -(2.0 ** -14)),
                  ("IDH", 0.5), ("IDQ", -0.25), ("I7N", -7.5), ("IBG", M19), ("ID2", 2048.0), ("ID8", 8192.0)):
        act(X(nm), X("IDP"), F.Copy, scale=c)
    vcp(X("IDF"), X("IDP"))
    vcp(X("BF"), X("BM"))
    vcp(X("WSF"), X("WSB"))
    act(X("BMH"), X("BM"), F.Copy, scale=-0.5)
    act(X("BMW"), X("BM"), F.Copy, scale=128.0)
    act(X("WSM"), X("WSB"), F.Copy, scale=-0.5)
    act(X("WSG"), X("WSB"), F.Copy, scale=16384.0)
    JS = min([c[3] for c in C3 if c[3]])
    if JS < 16:
        gsel(X("BMJ"), X("BMH"), [[0, 8], [-1, 16]], A.is_ge, JS - 1, 0)

    def turn(name, lo, hi):
        n = hi - lo
        P, P2 = X("b5", 256, 384, 1, n), X("b5", 384, 512, 1, n)
        mm([(P, X("CF", lo, hi), X("IDF")), (P, X("HB", lo, hi), X("IDN")), (P2, X("HB", lo, hi), X("IDP"))])
        aff("KT", X(name, 0, 128, 1, n), P, -1.0, -2048.0)
        aff("KT", X(name, 128, 256, 1, n), P2, -(2.0 ** -14), 0.0)

    def forms(src, lo, hi):
        vts(X("CF", lo, hi), X(src, lo, hi), -2048.0, None, A.add)
        vts(X("C16", lo, hi), X("CF", lo, hi), 2048.0, None, A.add)
        vts(X("HF", lo, hi), X("CF", lo, hi), 2048 + 24576 - 7.5, None, A.add)
        vts(X("HB", lo, hi), X("HF", lo, hi), -24576.0, None, A.add)
        for h in SPR:
            l, e = SPR[h]
            e = "gggg" if src == "REQ" else e
            if not lo < h <= hi:
                continue
            if e == "p":
                n = h - l
                turn("KS", l, h)
                for a in range(0, 16 * n, 1024):
                    for b in (0, 512):
                        x = X("EB", a + b, a + b + 512, 1, n)
                        mm([(X("b1", b, b + 512), X("KS", c, c + 128, 1, n), x) for c in (0, 128)])
                    act(X("CKB", 16 * l + a, 16 * l + a + 1024), X("b1", 0, 1024), F.Identity, bias=OFF, scale=-1.0)
                continue
            P = X("b5", l, h)
            mm([(P, X("IDF"), X("CF", l, h)), (P, X("IDN"), X("HB", l, h)), (P, X("IDK"), X("HB", l, h))])
            aff("TC", X("TC", l, h), P, 1.0, 2048 + OFF)
            o, i = [ap(X("CKB", 16 * l + j, 16 * h, 16)) for j in range(16)], ap(X("TC", l, h))
            for j in range(0, 16, 4):
                wr = [X("CKB", 16 * l + k, 16 * h, 16) for k in range(j, j + 4)]
                if e[j // 4] == "g":
                    add("g", [(lambda x=x, i=i, n=h - l: g.affine_select(x, i, [[0, n]], A.is_equal, 0.0, 0, 0)) for x in o[j:j + 4]],
                        4 * (GF + 2 * (h - l) * CYC), [X("TC", l, h)], wr)
                else:
                    add("s", [(lambda x=x, i=i: g.scalar.activation(x, i, F.Copy)) for x in o[j:j + 4]],
                        4 * (SF + (h - l) * CYC), [X("TC", l, h)], wr)
        if lo < KH <= hi:
            turn("KT", KL, KH)

    for lo, hi in CN:
        forms("REQ", lo, hi)

    for k in range(len(UNP)):
        l0, h0 = UB[k], UB[k + 1]
        vts(X("A2", l0, h0), X("REC", l0, h0), -2047.5, M35, A.add, A.add)
        act(X("XX", l0, h0), X("A2", l0, h0), F.Identity, bias=-M23, scale=2.0 ** -12)
        P, P2 = X(("b1", "b2", "b4")[k % 3]), X(("b3", "b6", "b7")[k % 3])
        ht = [(P2, X("IDN"), X("HT", l0, h0)), (P2, X("IDK"), X("HT", l0, h0))]
        if UM[k] == "d":
            mm([(P, X("ID2"), X("ONES", 0, 512)), (P, X("ID4"), X("XX", l0, h0))])
            vtt(X("DC", l0, h0), X("REC", l0, h0), P, A.subtract)
            vts(X("HH", l0, h0), X("DC", l0, h0), 2048 + 24576 - 7.5, None, A.add)
            vts(X("HT", l0, h0), X("HH", l0, h0), -24576.0, None, A.add)
            mm([(P2, X("IDF"), X("DC", l0, h0))] + ht)
            act(X("TT", l0, h0), P2, F.Identity, bias=2048 + OFF)
            continue
        mm([(P, X("ID7"), X("ONES", 0, 512)), (P, X("ID4"), X("XX", l0, h0))])
        vtt(X("A2", l0, h0), X("REC", l0, h0), P, A.subtract)
        if UM[k] == "s":
            act(X("A1", l0, h0), X("A2", l0, h0), F.Identity, bias=M27)
            act(X("HT", l0, h0), X("A1", l0, h0), F.Identity, bias=-M27 - 32)
        else:
            vts(X("HT", l0, h0), X("A2", l0, h0), M27, -M27 - 32, A.add, A.add)
        mm(ht)
        vtt(X("TT", l0, h0), X("A2", l0, h0), P2, A.add)
    vts(X("THH"), X("TH"), 0.5, None, A.mult)
    vcp(X("KF"), X("MUL"))
    vts(X("PR"), X("PRI"), 15, None, A.bitwise_and)
    vts(X("ODC"), X("PR", 0, 1), 2.0, 1.0, A.mult, A.add)
    vts(X("OB"), X("PR", 0, 1), 256.0, 128.0, A.mult, A.add)
    vts(X("OD"), X("IDP"), X("ODC"), None, A.mult)
    vts(X("R16"), X("PR"), 16.0, None, A.mult)
    vtt(X("PI"), X("R16"), X("I256"), A.add)
    vts(X("BASE"), X("PI"), 7.5, None, A.add)
    vtt(X("DUM"), X("PR"), X("I16"), A.add)
    k = SB // 16
    vcp(X("BASL", 0, k), X("BASE", 0, k))
    vcp(X("DUL", 0, k), X("DUM", 0, k))
    vts(X("BASL", k, 16), X("BASE", k, 16), -16.0 * SB, None, A.add)
    vts(X("DUL", k, 16), X("DUM", k, 16), -16.0 * SB, None, A.add)
    vts(X("THS"), X("TH"), -0.5, 0.25, A.mult, A.add)
    vcp(X("b0", 0, 256), X("WT"))

    me = T.rank_of(core)
    GR = [(0, SP), (SP, 256)]
    for t in range(STEPS):
        last, first = t == STEPS - 1, len(ops)
        dst = T.cores[(me + 1 + t % 3) % len(T.cores)]
        rid, pid, _ = topo.addr(dst)
        msk, ne = topo.mask(core, dst), len(topo.engines(core, dst))
        CP, CA, VN, VA = ["%s%d" % (x, t) for x in ("CP", "CA", "VN", "VA")]

        def send(m, out, src, t=t, rid=rid, pid=pid, msk=msk, ne=ne):
            ls, rs = "%s%dl" % (m, t), "%s%dr" % (m, t)
            tok = ("sent" + ls, 0, 1, 1, 128)
            add("g", [lambda: g.remote_dma(ap(out), ap(src), T.sem[rs], T.sem[ls], pid, rid, msk)], SND, [src], [tok], "r", SND, ls, ne,
                chain("send"))
            ops[-1]["tag"] = "gsend." + m
            add("n", [], ARR + ARC * size(src), [tok], [out], "n", 0.0, rs, ne)

        for lo, hi in C1:
            el, eh = 16 * lo, 16 * hi
            names = ind(X("TT", 0, W), X("C16", lo, hi))
            if not KL <= lo < KH:
                vtt(X("U1", el, eh), names, X("CKB", el, eh), A.subtract)
                act(X("AB", el, eh), X("U1", el, eh), F.Abs, bias=4080.0, scale=-16384.0)
            else:
                gather("s", X("A1", el, eh), names)
        for l0 in range(16 * KL, 16 * KH, AU):
            o = (l0 - 16 * KL) % 1024
            for l in range(l0, l0 + AU, PU):
                P = X("b1", o + l - l0, o + l - l0 + PU)
                e = X("EB", l - 16 * KL, l + PU - 16 * KL, 1, KH - KL)
                mm([(P, X("KT", 0, 128, 1, KH - KL), e), (P, X("KT", 128, 256, 1, KH - KL), e), (P, X("I32"), X("A1", l, l + PU))])
            act(X("AB", l0, l0 + AU), X("b1", o, o + AU), F.Abs, bias=4080.0 + OFF * 16384, scale=-16384.0)
        for lo, hi in C1S:
            n = 16 * (hi - lo)
            el, eh = 16 * lo, 16 * hi
            vscan(X("MN", el, eh), X("MSN", 0, n), X("AB", el, eh), A.max, A.min)
            mn = X("MN", el + 15, eh, 16)
            if silu:
                vts(X("M2", lo, hi), mn, M27, -M27, A.add, A.add)
                mn = X("M2", lo, hi)
            if hi in CPV:
                vtt(X("CT", lo, hi), X("CF", lo, hi), mn, A.subtract)
                vts(X(CP, lo, hi), X("CT", lo, hi), 2048.0 + 4080.0, None, A.add)
            else:
                P = X(("b3", "b6")[lo // 64 % 2], lo, hi)
                mm([(P, X("IDF"), X("CF", lo, hi)), (P, X("IDN"), mn)])
                vts(X(CP, lo, hi), P, 2048.0 + 4080.0, None, A.add)
            if hi in SC:
                send("e" if hi == 256 else "c", X(CA, SC[hi], hi), X(CP, SC[hi], hi))
        if not last:
            P = X("b4", 0, 256)
            mm([(P, X("IDF"), X("CF")), (P, X("IDN"), X("HB")), (P, X("IDK"), X("HB"))], True, False)
            mm([(P, X("IDM"), X("M2") if silu else X("MN", 15, W, 16))], False, True)
            aff("TV", X("TV"), P, 1.0, 2048 + OFF + 4080.0 / 16384)
        for lo, hi, e in C2:
            n = 16 * (hi - lo)
            el, eh = 16 * lo, 16 * hi
            gather(e, X("XG", el, eh), ind(X("XX", 0, W), X(CP, lo, hi)), chain("x" + e))
            vscan(X("MX", el, eh), X("MSX", 0, n), X("XG", el, eh), A.mult, A.max)
            vscan(X("MI", el, eh), X("MSN", 0, n), X("XG", el, eh), A.max, A.min)
        for lo, hi, e in CZ:
            el, eh = 16 * lo, 16 * hi
            if e == "v":
                vtt(X("CT", lo, hi), X("MX", el + 15, eh, 16), X("MI", el + 15, eh, 16), A.add)
                vts(X("FF", lo, hi), X("CT", lo, hi), 0.5, -128.25, A.mult, A.add)
                vtt(X("WZ", lo, hi), X("FF", lo, hi), X("b0", lo, hi), A.mult)
                vcp(X("Z", lo, hi), X("FF", lo, hi))
                continue
            P = X(("b6", "b3")[lo // 64 % 2], 256 + lo, 256 + hi)
            mm([(P, X("IDQ"), X("ONES", 0, hi - lo)), (P, X("IDH"), X("MX", el + 15, eh, 16)), (P, X("IDH"), X("MI", el + 15, eh, 16))])
            vts(X("Z", lo, hi), P, M23, -M23 - 128, A.add, A.add)
            vtt(X("WZ", lo, hi), X("Z", lo, hi), X("b0", lo, hi), A.mult)
        for lo, hi in CV:
            P = X("b2", lo, hi)
            mm([(P, X("IDN"), X("AIM", lo, hi)), (P, X("IDP"), X("Z", lo, hi))])
            act(X(VN, lo, hi), P, F.Abs, bias=128.0)
        for lo, hi in GR:
            wl, wh = lo // 16, hi // 16
            P = X("b7", 480 + wl, 480 + wh)
            mm([(P, X("I7N"), X("ONES", 0, wh - wl))] + [(P, sel("WSF", r), X("WZ", lo + r, hi, 16)) for r in range(16)])
            vts(X("FU", wl, wh), P, M27, -M27, A.add, A.add)
            nn = X(VN, 256 + wl, 256 + wh)
            vtt(nn, P, X("FU", wl, wh), A.subtract)
            if lo == 0:
                vtt(X("PI", wl, wh), nn, X("BASE", wl, wh), A.add)
                vcp(X("P16", wl, wh), X("PI", wl, wh))
            else:
                for w in range(wl, wh):
                    vts(X("P16", w, w + 1), X("b7", 480 + w, 481 + w), X("FU", w, w + 1), X("BASE", w, w + 1), A.subtract, A.add)
        for k in range(len(SV)):
            lo, hi = SV[k]
            hi += 16 if hi == 256 else 0
            send("uvw"[k - len(SV)], X(VA, lo, hi), X(VN, lo, hi))
        for lo, hi in GR:
            vcp(ind(X("XX", 0, W), X("P16", lo // 16, hi // 16)), X(VN, lo, hi))
            if not last:
                put(ENG["OWN"][lo > 0], ind(X("TT", 0, W), X("P16", lo // 16, hi // 16)), X("TV", lo, hi))
        if last:
            vts(X("ZO"), X("Z"), 128.0, None, A.add)
            dma("y", T.yz[:], T.ZO[:], 2.5, [X("ZO")], [("yz", 0, 1, 1, 128)])
        for lo, hi in CN:
            wz, wt = X("WZ", lo, hi), X("WT", lo, hi)
            P = X("b5", lo, hi)
            mm([(P, X("BF"), wz), (P, X("BMW"), wt)])
            aff("QQ", X("QQ", lo, hi), P, 1.0, M19 - 2047.5)
            P = X("b5", 256 + lo, 256 + hi)
            mm([(P, X("IBG"), X("ONES", 0, hi - lo)), (P, X("IDN"), X("QQ", lo, hi)), (P, X("BF"), wz), (P, X("BMW"), wt)])
            act(X("SQ", lo, hi), P, F.Square)
            aff("KU", X("KU", lo, hi), P, X("KF"), X("OB"))
            vts(X("FF", lo, hi), X("SQ", lo, hi), 1.0 / 32, -0.375, A.mult, A.add)
            P = X("b3", lo, hi)
            mm([(P, X("I32"), X("KU", lo, hi)), (P, X("OD"), X("Z", lo, hi))])
            vtt(X("RR", lo, hi), X("FF", lo, hi), P, A.add)
            vts(X("CC", lo, hi), X("RR", lo, hi), 4095, None, A.bitwise_and)
            if last:
                vcp(X("YC", lo, hi), X("CC", lo, hi))
            else:
                forms("CC", lo, hi)
        if last:
            dma("y", T.yc[:], T.YC[:], 2.5, [X("YC")], [("yc", 0, 1, 1, 128)])
        if not last:
            vts(X("CG"), X(CA), -2048.0, None, A.add)
            vts(X("HG"), X("CG"), 2048 + 24576 - 7.5, None, A.add)
            vts(X("HA"), X("HG"), -24576.0, None, A.add)
            P = X("b3", 256, 512)
            mm([(P, X("IDF"), X("CG")), (P, X("IDN"), X("HA")), (P, X("IDK"), X("HA"))])
            aff("TA", X("TA"), P, 1.0, 2048 + OFF)
        for lo, hi in SV:
            hi = max([lo] + [c[1] for c in C3 if c[1] - c[0] > 32 and c[3] and c[1] <= hi])
            if hi == lo:
                continue
            if ENG["VAP"] == "v":
                vcp(X("b0", 256 + lo, 256 + hi), X(VA, lo, hi))
            else:
                act(X("b0", 256 + lo, 256 + hi), X(VA, lo, hi), F.Copy)
        vtt(X("PD"), X(VA, 256, 272), X("BASL" if last else "BASE"), A.add)
        for c in range(len(C3)):
            lo, hi, e, js = C3[c]
            m = hi - lo
            el, eh = 16 * lo, 16 * hi
            va = X(VA, lo, hi)
            for l, h, e in CG:
                if lo <= l < hi:
                    gather(e, X("XA", 16 * l, 16 * h), ind(X("XX", 0, W), X(CA, l, h)), chain("x" + e))
            D = X("b%d" % (6, 4, 2, 7, 6)[c], 0, m)
            xa = [X("XA", el + j, eh, 16) for j in range(16)]
            mx = [X("MXA", el + m * j, el + m * j + m) for j in range(16)]
            if js:
                mm([(D, sel("WSM", j), xa[j]) for j in range(js)], True, False)
            runs = ([(0, js // 2), (js // 2, js)] if hi < 256 else [(0, 6), (6, 12), (12, 16)]) + [(j, min(j + 512 // m, 16)) for j in range(js, 16, 512 // m)]
            for j0, j1 in runs:
                if j1 == j0:
                    continue
                if j1 <= js:
                    vtts([(mx[j], xa[j], va if m <= 32 else X("b0", 256 + lo, 256 + hi)) for j in range(j0, j1)], A.max)
                else:
                    b = "b1"
                    mm([x for j in range(j0, j1) for x in ((X(b, m * (j - j0), m * (j - j0 + 1)), X("IDP"), xa[j]),
                                                           (X(b, m * (j - j0), m * (j - j0 + 1)), X("IDN"), va))])
                    act(X("MXA", el + m * j0, el + m * j1), X(b, 0, m * (j1 - j0)), F.Abs, scale=0.5)
                mm([(D, X("BMH" if js == 16 else "BMJ"), va)] * (j0 == 0 and js > 0) +
                   [(D, sel("WSB", j), mx[j]) for j in range(j0, j1)], j0 == 0 and js == 0, j1 == 16)
            fe = ENG["FL"][0 if hi <= SB else 1]
            if fe == "v":
                vts(X("FL", lo, hi), D, X("THH"), -15.0 / 32, A.is_ge, A.add)
            else:
                act(X("FL", lo, hi), D, F.Sign, bias=X("THS"))
            if hi not in (SB, 256):
                continue
            lo = 0 if hi == SB else SB
            wl, wh = lo // 16, hi // 16
            P = X("b6", 480 + wl, 480 + wh)
            mm([(P, X("ID8"), X("ONES", 0, wh - wl))] * (fe == "s") + [(P, sel("WSG", r), X("FL", lo + r, hi, 16)) for r in range(16)])
            dum = "DUL" if last else "DUM"
            if lo == 0:
                vtt(X("OF", wl, wh), P, X("PD", wl, wh), A.max)
                vtt(X("OG", wl, wh), X("OF", wl, wh), X(dum, wl, wh), A.min)
                vcp(X("O16", wl, wh), X("OG", wl, wh))
            else:
                for w in range(wl, wh):
                    vts(X("O16", w, w + 1), X("b6", 480 + w, 481 + w), X("PD", w, w + 1), X(dum, w, w + 1), A.max, A.min)
            if not last:
                put(ENG["ARR"][lo > 0], ind(X("TT"), X("O16", wl, wh)), X("TA", lo, hi))
        for lo, hi in ((0, SB), (SB, 256)):
            vcp(ind(X("XX", 16 * lo if last else 0, WP), X("O16", lo // 16, hi // 16)), X(VA, lo, hi))
            if last:
                dma("y" if lo == 0 else "s", T.yx[:, 16 * lo:16 * hi], T.XX[:, 16 * lo:16 * hi], 2.0 + (hi - lo) * 0.012,
                    [X("XX", 16 * lo, 16 * hi)], [("yx%d" % lo, 0, 1, 1, 128)])
        at = {ops[i]["tag"]: i for i in range(first, len(ops))}
        for run in RUNS:
            run = [at[x] for x in run.split() if x in at]
            for a, b in zip(run, run[1:]):
                ops[b]["after"].append(a)
    return ops, q


def rank_program(g, core, T, topo):
    if T.rank_of(core) is None:
        return
    ops, q = build(g, T, core, topo)
    if "o" not in ORDER:
        preds = plan(ops)
        order, start, end, extra = schedule(ops, preds)
        for i in range(len(ops)):
            for j in extra[i]:
                preds[i][j] = True
        ORDER["o"] = (order, preds)
    order, preds = ORDER["o"]
    pos = {}
    for i in order:
        pos[i] = len(pos)
    semof = {"v": "sv", "s": "ss", "t": "st", "g": "sg"}
    cnt, done, clock, final = {}, {}, {}, {}
    known = {e: {} for e in q}
    for i in order:
        o = ops[i]
        e = o["e"]
        if e == "n":
            done[i] = (o["sem"], o["val"])
            final[o["sem"]] = o["val"]
            clock[i] = {}
            continue
        kn = known[e]
        for j in sorted(preds[i], key=lambda x: -pos[x]):
            if not preds[i][j]:
                continue
            s, v = done[j]
            if kn.get(s, 0) >= v:
                continue
            q[e].wait_ge(T.sem[s], v)
            kn[s] = v
            for a, b in clock[j].items():
                if kn.get(a, 0) < b:
                    kn[a] = b
        clock[i] = dict(kn)
        if o["k"] == "c":
            s = semof[e]
            for f in o["f"]:
                f().then_inc(T.sem[s], 1)
                cnt[s] = cnt.get(s, 0) + 1
            done[i] = (s, cnt[s])
        elif o["k"] == "d":
            o["f"][0]().then_inc(T.sem[o["sem"]], 16)
            done[i] = (o["sem"], 16)
        else:
            o["f"][0]()
            done[i] = (o["sem"], o["val"])
        final[done[i][0]] = done[i][1]
        clock[i][done[i][0]] = done[i][1]
    for s in sorted(final):
        if known["g"].get(s, 0) < final[s]:
            g.wait_ge(T.sem[s], final[s])
